import numpy as np
import ml_dtypes


def mxq(x, axis, fmt="e4m3"):
    dtype, down = {"e4m3": (ml_dtypes.float8_e4m3fn, 7), "e5m2": (ml_dtypes.float8_e5m2, 14)}[fmt]
    v = np.moveaxis(np.asarray(x, np.float32).astype(ml_dtypes.bfloat16).astype(np.float64), axis, -1)
    blocks = v.reshape(v.shape[:-1] + (-1, 32))
    amax = np.abs(blocks).max(-1, keepdims=True)
    byte = np.maximum(np.where(amax > 0, np.frexp(amax)[1] - 1 + 127, 0) - down, 1)
    scale = np.exp2(byte - 127.0)
    codes = (blocks / scale).astype(np.float32).astype(dtype).astype(np.float64)
    return np.moveaxis((codes * scale).reshape(v.shape), -1, axis)


WIDE = False


def mx_kscale(k):
    if not WIDE:
        return np.ones(k)
    levels = np.array([10, -10, 5, -5, 0])
    if k % 512:
        return np.exp2(np.random.permutation(np.resize(levels, k // 32))).repeat(32)
    a = np.empty((k // 512, 16))
    for p in range(k // 512):
        a[p, :8] = np.random.permutation(np.resize(levels, 8))
        for g in range(8):
            far = levels[np.abs(levels - a[p, g]) >= 10]
            a[p, g + 8] = far[np.random.randint(len(far))]
    return np.exp2(a.ravel()).repeat(32)


def f64(x):
    return np.asarray(x).astype(np.float64)


def striped8(idx):
    return np.concatenate([x.reshape(-1, 16).T for x in idx]).astype(np.uint16)


def runs(offs, k):
    lists = np.stack([offs[16 * r : 16 * r + 16].T.reshape(-1) for r in range(8)]).astype(np.int64)
    return lists[np.arange(k) % 512 // 64]


def pack_weight(w):
    k, n = w.shape
    w = f64(np.asarray(w, np.float32).astype(ml_dtypes.bfloat16)).reshape(k // 32, 32, n)
    amax = np.abs(w).max(1)
    byte = np.clip(np.where(amax > 0, np.frexp(amax)[1] - 1 + 127 - 7, 1), 1, 254)
    scaled = (w * np.exp2(127.0 - byte)[:, None, :]).reshape(k, n).astype(np.float32)
    words = np.ascontiguousarray(scaled.reshape(k // 512, 128, 4, n).transpose(0, 1, 3, 2)).astype(ml_dtypes.float8_e4m3fn).view(np.uint8)
    return words, np.ascontiguousarray(byte.astype(np.uint8).reshape(k // 512, 16, n))


def unpack_weight(words, scales):
    g, p, n, _ = words.shape
    vals = np.ascontiguousarray(words).view(ml_dtypes.float8_e4m3fn).astype(np.float64) * np.repeat(np.exp2(scales.astype(np.float64) - 127.0), 8, axis=1)[..., None]
    return vals.transpose(0, 1, 3, 2).reshape(g * 512, n)


K, T, S, H, W, C = 512, 2048, 512, 512, 256, 512


def setup_inputs():
    n = np.random.standard_normal
    s = mx_kscale(K)[:, None]
    packed_xT = pack_weight(n((K, T)) * s)
    perm = np.stack([np.random.permutation(S) for _ in range(8)])
    return {
        "x_words": packed_xT[0],
        "x_scales": packed_xT[1],
        "w1": (n((K, H)) / np.sqrt(K) / s).astype(np.float32),
        "gs": (np.random.uniform(0.5, 1.5, (K, 1)) / s).astype(np.float32),
        "offs": striped8(np.random.randint(0, T, (8, S))),
        "n1": striped8(perm[:, :W]),
        "n2": striped8(perm[:, W:]),
        "cand": striped8(np.random.randint(0, T, (8, C))),
        "n3": striped8(np.stack([np.random.permutation(S) for _ in range(8)])),
        "n4": striped8(np.stack([np.random.permutation(S) for _ in range(8)])),
    }


def reference(x_words, x_scales, w1, gs, offs, n1, n2, cand, n3, n4):
    x_cand = unpack_weight(x_words, x_scales)[np.arange(K)[:, None], runs(cand, K)]
    xq = unpack_weight(x_words, x_scales)[np.arange(K)[:, None], runs(offs, K)]
    y = mxq(f64(w1), 0, "e4m3").T @ xq
    pa = y[np.arange(H)[:, None], runs(n1, H)]
    pb = y[np.arange(H)[:, None], runs(n2, H)]
    rb = pa * pb
    ra = pa + pb
    ds = np.zeros((H, S))
    ds[np.arange(H)[:, None], runs(n1, H)] = ra
    dt = ds.copy()
    dt[np.arange(H)[:, None], runs(n2, H)] = rb
    z = f64(gs) * dt
    s = 0.0625 * ((x_cand.T @ mxq(z, 0, "e4m3")))
    pa2 = s[np.arange(C)[:, None], runs(n3, C)]
    pb2 = s[np.arange(C)[:, None], runs(n4, C)]
    mu = 0.3125 * (s + pa2 + pb2)
    return (s - mu) / (np.sqrt((pa2 - mu) ** 2 + (pb2 - mu) ** 2 + 0.25))

@@ -1,0 +1,216 @@
+import math
+from contextlib import ExitStack
+
+import concourse.mybir as mybir
+
+K, T, S, H, W, C = 512, 2048, 512, 512, 256, 512
+FLOPS = 2 * K * H * S + 2 * K * C * S
+
+F32 = mybir.dt.float32
+BF16 = mybir.dt.bfloat16
+I32 = mybir.dt.int32
+U32 = mybir.dt.uint32
+U16 = mybir.dt.uint16
+U8 = mybir.dt.uint8
+FP8X4 = mybir.dt.float8_e4m3fn_x4
+ALU = mybir.AluOpType
+ACT = mybir.ActivationFunctionType
+
+P = 128
+PACK = 4
+HALF = 256
+
+
+def tile_picked_hcandbondstd_none_p_kernel(tc, x_words, x_scales, w1, gs, offs, n1, n2, cand, n3, n4, out):
+    nc = tc.nc
+    with ExitStack() as ctx:
+        keep = ctx.enter_context(tc.tile_pool(name="keep", bufs=1))
+        ring = ctx.enter_context(tc.tile_pool(name="ring", bufs=3))
+        psum = ctx.enter_context(tc.psum_pool(name="psum", bufs=1))
+
+        def load_list(dram, name):
+            tile = keep.tile(list(dram.shape), U16, name=name)
+            nc.sync.dma_start(tile[:], dram)
+            return tile
+
+        table_scales = keep.tile([P, T], U8, name="table_scales")
+        nc.vector.memset(table_scales[:].bitcast(I32), 0)
+        one = keep.tile([P, 1], F32, name="one")
+        nc.vector.memset(one[:], 1.0)
+
+        offs_t = load_list(offs, "offs_t")
+        warm = keep.tile([P, 1], F32, name="warm")
+        nc.scalar.activation(warm[:], one[:], ACT.Abs_reciprocal_sqrt)
+
+        w_rows = w1.rearrange("(p j) h -> p j h", j=PACK)
+        w_raw = []
+        for u in range(2):
+            piece = keep.tile([P, PACK, HALF], F32, name="w_raw%d" % u)
+            nc.sync.dma_start(piece[:], w_rows[:, :, u * HALF : (u + 1) * HALF])
+            w_raw.append(piece)
+            if u == 0:
+                scale_rows = x_scales[0].rearrange("(r e) n -> e r n", e=2)
+                for e in range(2):
+                    nc.sync.dma_start(table_scales[e:P:16, :].bitcast(I32), scale_rows[e].bitcast(I32))
+        table_words = keep.tile([P, T], U32, name="table_words")
+        nc.sync.dma_start(table_words[:].bitcast(I32), x_words[0].rearrange("p n t -> p (n t)").bitcast(I32))
+        cand_t = load_list(cand, "cand_t")
+        n1_t = load_list(n1, "n1_t")
+        n2_t = load_list(n2, "n2_t")
+        n3_t = load_list(n3, "n3_t")
+        n4_t = load_list(n4, "n4_t")
+        gs_t = keep.tile([P, PACK], F32, name="gs_t")
+        nc.gpsimd.dma_start(gs_t[:], gs.rearrange("(p t) o -> p (t o)", t=PACK))
+
+        def place_scale_rows(src, name):
+            plane = keep.tile([P, S], U8, name=name, align_bytes=64)
+            nc.vector.tensor_copy(plane[:].bitcast(I32), src[:].bitcast(I32))
+            for e in range(2):
+                nc.scalar.dma_start(plane[2 + e : P : 32, :].bitcast(I32), src[16 + e : P : 32, :].bitcast(I32))
+            return plane
+
+        x_bytes = keep.tile([P, S], U8, name="x_bytes")
+        nc.vector.tensor_copy(x_bytes[:], table_scales[:].indirect(offs_t[:]))
+        x_plane = place_scale_rows(x_bytes, "x_plane")
+
+        w_grouped = keep.tile([P, PACK, P, PACK], BF16, name="w_grouped", align_bytes=64)
+        m_half = P // 2
+        for u in range(2):
+            dst = w_grouped[:, :, u * m_half : (u + 1) * m_half, :].rearrange("p t m j -> p m t j")
+            src = w_raw[u][:].rearrange("p j (m t) -> p m t j", t=PACK)
+            if u == 0:
+                nc.scalar.copy(dst, src)
+            else:
+                nc.vector.tensor_copy(dst, src)
+        w_codes = keep.tile([P, H], U32, name="w_codes", align_bytes=64)
+        w_plane = keep.tile([P, H], U8, name="w_plane", align_bytes=64)
+        nc.vector.quantize_mx(w_codes[:].bitcast(FP8X4), w_plane[:], w_grouped[:].rearrange("p t m j -> p (t m j)"))
+
+        x_codes = keep.tile([P, S], U32, name="x_codes", align_bytes=64)
+        nc.vector.tensor_copy(x_codes[:], table_words[:].indirect(offs_t[:]))
+
+        y = []
+        for t in range(PACK):
+            cols = slice(t * P, (t + 1) * P)
+            bank = psum.tile([P, S], F32, name="y_bank%d" % t)
+            nc.tensor.matmul_mx(bank[:], lhsT=w_codes[:, cols].bitcast(FP8X4), lhsT_scale=w_plane[:, cols],
+                                rhs=x_codes[:].bitcast(FP8X4), rhs_scale=x_plane[:], start=True, stop=True)
+            y_t = keep.tile([P, S], F32, name="y%d" % t)
+            nc.scalar.copy(y_t[:], bank[:])
+            y.append(y_t)
+
+        c_bytes = keep.tile([P, C], U8, name="c_bytes")
+        nc.vector.tensor_copy(c_bytes[:], table_scales[:].indirect(cand_t[:]))
+        c_bytes_dealt = keep.tile([P, C], U8, name="c_bytes_dealt")
+        nc.vector.tensor_copy(c_bytes_dealt[:].rearrange("p (t m) -> p m t", t=PACK), c_bytes[:].rearrange("p (m t) -> p m t", t=PACK))
+        c_plane = place_scale_rows(c_bytes_dealt, "c_plane")
+
+        z_grouped = [keep.tile([P, HALF, PACK], BF16, name="z_grouped%d" % u, align_bytes=64) for u in range(2)]
+        pa, pb, dt = {}, {}, {}
+
+        def fetch_a(t):
+            pa[t] = keep.tile([P, W], F32, name="pa%d" % t, tag="late" if t == PACK - 1 else "pa%d" % t)
+            nc.vector.tensor_copy(pa[t][:], y[t][:].indirect(n1_t[:]))
+
+        def fetch_b(t):
+            pb[t] = keep.tile([P, W], F32, name="pb%d" % t)
+            nc.vector.tensor_copy(pb[t][:], y[t][:].indirect(n2_t[:]))
+
+        def put_sum(t):
+            dt[t] = keep.tile([P, S], F32, name="dt%d" % t)
+            nc.vector.tensor_tensor(dt[t][:].indirect(n1_t[:]), pa[t][:], pb[t][:], ALU.add)
+
+        def put_product(t):
+            nc.vector.tensor_tensor(dt[t][:].indirect(n2_t[:]), pa[t][:], pb[t][:], ALU.mult)
+            for u in range(2):
+                nc.scalar.activation(z_grouped[u][:, :, t], dt[t][:, u * HALF : (u + 1) * HALF], ACT.Copy, scale=gs_t[:, t : t + 1])
+
+        fetch_a(0)
+        fetch_b(0)
+        for t in range(PACK):
+            if t + 1 < PACK:
+                fetch_a(t + 1)
+            put_sum(t)
+            if t + 1 < PACK:
+                fetch_b(t + 1)
+            put_product(t)
+
+        c_words = keep.tile([P, C], U32, name="c_words", tag="late")
+        nc.vector.tensor_copy(c_words[:], table_words[:].indirect(cand_t[:]))
+        c_codes = keep.tile([P, C], U32, name="c_codes", align_bytes=64)
+        nc.vector.tensor_copy(c_codes[:].rearrange("p (t m) -> p m t", t=PACK), c_words[:].rearrange("p (m t) -> p m t", t=PACK))
+
+        z_codes = keep.tile([P, S], U32, name="z_codes", align_bytes=64)
+        z_plane = keep.tile([P, S], U8, name="z_plane", align_bytes=64)
+        for u in range(2):
+            cols = slice(u * HALF, (u + 1) * HALF)
+            nc.vector.quantize_mx(z_codes[:, cols].bitcast(FP8X4), z_plane[:, cols], z_grouped[u][:].rearrange("p n t -> p (n t)"))
+
+        banks, windows = [], []
+        for t in range(PACK):
+            cols = slice(t * P, (t + 1) * P)
+            bank = psum.tile([P, S], F32, name="s_bank%d" % t)
+            nc.tensor.matmul_mx(bank[:], lhsT=c_codes[:, cols].bitcast(FP8X4), lhsT_scale=c_plane[:, cols],
+                                rhs=z_codes[:].bitcast(FP8X4), rhs_scale=z_plane[:], start=True, stop=True)
+            window = keep.tile([P, S], F32, name="window%d" % t)
+            nc.scalar.copy(window[:], bank[:])
+            banks.append(bank)
+            windows.append(window)
+
+        out_rows = out.rearrange("(p t) n -> t p n", t=PACK)
+        units = [(t, u) for t in range(PACK) for u in range(2)]
+        st = {}
+
+        def gather_first(i):
+            t, u = units[i]
+            a = ring.tile([P, HALF], F32, name="a")
+            nc.vector.tensor_copy(a[:], windows[t][:].indirect(n3_t[:, 16 * u : 16 * (u + 1)]))
+            st[i] = {"a": a}
+
+        def gather_second(i):
+            t, u = units[i]
+            both = ring.tile([P, HALF], F32, name="both")
+            nc.vector.tensor_tensor(both[:], windows[t][:].indirect(n4_t[:, 16 * u : 16 * (u + 1)]), st[i]["a"][:], ALU.add)
+            st[i]["both"] = both
+
+        def linear(i):
+            t, u = units[i]
+            own = banks[t][:, u * HALF : (u + 1) * HALF]
+            both = st[i]["both"]
+            diff = ring.tile([P, HALF], F32, name="diff")
+            nc.vector.scalar_tensor_tensor(diff[:], both[:], -0.5, st[i]["a"][:], ALU.mult, ALU.add)
+            mean = ring.tile([P, HALF], F32, name="mean")
+            nc.vector.scalar_tensor_tensor(mean[:], both[:], 0.6, own, ALU.mult, ALU.subtract)
+            num = ring.tile([P, HALF], F32, name="num")
+            nc.vector.scalar_tensor_tensor(num[:], both[:], -0.3125 / 0.6875, own, ALU.mult, ALU.add)
+            diff2 = ring.tile([P, HALF], F32, name="diff2")
+            nc.scalar.activation(diff2[:], diff[:], ACT.Square, scale=math.sqrt(0.5) / 8)
+            mean2 = ring.tile([P, HALF], F32, name="mean2")
+            nc.scalar.activation(mean2[:], mean[:], ACT.Square, scale=math.sqrt(0.5) * 0.625 / 16)
+            st[i]["num"], st[i]["diff2"], st[i]["mean2"] = num, diff2, mean2
+
+        def spread(i):
+            den = ring.tile([P, HALF], F32, name="den")
+            nc.vector.tensor_tensor(den[:], st[i]["diff2"][:], st[i]["mean2"][:], ALU.add)
+            inv = ring.tile([P, HALF], F32, name="inv")
+            nc.scalar.activation(inv[:], den[:], ACT.Abs_reciprocal_sqrt, bias=0.25)
+            st[i]["inv"] = inv
+
+        def finish(i):
+            t, u = units[i]
+            res = ring.tile([P, HALF], F32, name="res")
+            nc.vector.scalar_tensor_tensor(res[:], st[i]["num"][:], 0.6875 / 16, st[i]["inv"][:], ALU.mult, ALU.mult)
+            nc.sync.dma_start(out_rows[t][:, u * HALF : (u + 1) * HALF], res[:])
+
+        n = len(units)
+        for i in range(n + 2):
+            if i < n:
+                gather_first(i)
+            if 0 <= i - 2 < n:
+                spread(i - 2)
+            if i < n:
+                gather_second(i)
+            if 0 <= i - 1 < n:
+                linear(i - 1)
+            if 0 <= i - 2 < n:
+                finish(i - 2)

@@ -2,6 +2,7 @@ import math
 from contextlib import ExitStack
 
 import concourse.mybir as mybir
+from concourse.masks import make_identity
 
 K, T, S, H, W, C = 512, 2048, 512, 512, 256, 512
 FLOPS = 2 * K * H * S + 2 * K * C * S
@@ -19,6 +20,10 @@ ACT = mybir.ActivationFunctionType
 P = 128
 PACK = 4
 HALF = 256
+W_PIECES = ((0, 128), (128, 256), (256, 512))
+OWN = -0.3125 / 16
+SELF = 2.2 * OWN
+REST = 8 / 15 * OWN
 
 
 def tile_picked_hcandbondstd_none_p_kernel(tc, x_words, x_scales, w1, gs, offs, n1, n2, cand, n3, n4, out):
@@ -33,55 +38,60 @@ def tile_picked_hcandbondstd_none_p_kernel(tc, x_words, x_scales, w1, gs, offs, 
             nc.sync.dma_start(tile[:], dram)
             return tile
 
+        def bank_tile(b, name, width=S):
+            return psum.tile([P, width], F32, name=name, tag="bank%d" % b)
+
         table_scales = keep.tile([P, T], U8, name="table_scales")
-        nc.vector.memset(table_scales[:].bitcast(I32), 0)
+        nc.gpsimd.memset(table_scales[:].bitcast(I32), 0)
         one = keep.tile([P, 1], F32, name="one")
         nc.vector.memset(one[:], 1.0)
-
-        offs_t = load_list(offs, "offs_t")
         warm = keep.tile([P, 1], F32, name="warm")
         nc.scalar.activation(warm[:], one[:], ACT.Abs_reciprocal_sqrt)
 
+        offs_t = load_list(offs, "offs_t")
+        cand_t = load_list(cand, "cand_t")
         w_rows = w1.rearrange("(p j) h -> p j h", j=PACK)
         w_raw = []
-        for u in range(2):
-            piece = keep.tile([P, PACK, HALF], F32, name="w_raw%d" % u)
-            nc.sync.dma_start(piece[:], w_rows[:, :, u * HALF : (u + 1) * HALF])
+        for n, (lo, hi) in enumerate(W_PIECES):
+            piece = keep.tile([P, PACK, hi - lo], F32, name="w_raw%d" % n)
+            nc.sync.dma_start(piece[:], w_rows[:, :, lo:hi])
             w_raw.append(piece)
-            if u == 0:
+            if n == 0:
                 scale_rows = x_scales[0].rearrange("(r e) n -> e r n", e=2)
                 for e in range(2):
                     nc.sync.dma_start(table_scales[e:P:16, :].bitcast(I32), scale_rows[e].bitcast(I32))
         table_words = keep.tile([P, T], U32, name="table_words")
         nc.sync.dma_start(table_words[:].bitcast(I32), x_words[0].rearrange("p n t -> p (n t)").bitcast(I32))
-        cand_t = load_list(cand, "cand_t")
         n1_t = load_list(n1, "n1_t")
         n2_t = load_list(n2, "n2_t")
         n3_t = load_list(n3, "n3_t")
         n4_t = load_list(n4, "n4_t")
         gs_t = keep.tile([P, PACK], F32, name="gs_t")
         nc.gpsimd.dma_start(gs_t[:], gs.rearrange("(p t) o -> p (t o)", t=PACK))
+        ident = keep.tile([P, P], F32, name="ident")
+        make_identity(nc, ident[:])
 
         def place_scale_rows(src, name):
             plane = keep.tile([P, S], U8, name=name, align_bytes=64)
             nc.vector.tensor_copy(plane[:].bitcast(I32), src[:].bitcast(I32))
             for e in range(2):
-                nc.scalar.dma_start(plane[2 + e : P : 32, :].bitcast(I32), src[16 + e : P : 32, :].bitcast(I32))
+                nc.sync.dma_start(plane[2 + e : P : 32, :].bitcast(I32), src[16 + e : P : 32, :].bitcast(I32))
             return plane
 
         x_bytes = keep.tile([P, S], U8, name="x_bytes")
         nc.vector.tensor_copy(x_bytes[:], table_scales[:].indirect(offs_t[:]))
         x_plane = place_scale_rows(x_bytes, "x_plane")
 
+        c_bytes = keep.tile([P, C], U8, name="c_bytes")
+        nc.vector.tensor_copy(c_bytes[:], table_scales[:].indirect(cand_t[:]))
+        c_bytes_dealt = keep.tile([P, C], U8, name="c_bytes_dealt")
+        nc.vector.tensor_copy(c_bytes_dealt[:].rearrange("p (t m) -> p t m", t=PACK), c_bytes[:].rearrange("p (m t) -> p t m", t=PACK))
+        c_plane = place_scale_rows(c_bytes_dealt, "c_plane")
+
         w_grouped = keep.tile([P, PACK, P, PACK], BF16, name="w_grouped", align_bytes=64)
-        m_half = P // 2
-        for u in range(2):
-            dst = w_grouped[:, :, u * m_half : (u + 1) * m_half, :].rearrange("p t m j -> p m t j")
-            src = w_raw[u][:].rearrange("p j (m t) -> p m t j", t=PACK)
-            if u == 0:
-                nc.scalar.copy(dst, src)
-            else:
-                nc.vector.tensor_copy(dst, src)
+        for n, (lo, hi) in enumerate(W_PIECES):
+            nc.scalar.copy(w_grouped[:, :, lo // PACK : hi // PACK, :].rearrange("p t m j -> p m t j"),
+                           w_raw[n][:].rearrange("p j (m t) -> p m t j", t=PACK))
         w_codes = keep.tile([P, H], U32, name="w_codes", align_bytes=64)
         w_plane = keep.tile([P, H], U8, name="w_plane", align_bytes=64)
         nc.vector.quantize_mx(w_codes[:].bitcast(FP8X4), w_plane[:], w_grouped[:].rearrange("p t m j -> p (t m j)"))
@@ -92,24 +102,23 @@ def tile_picked_hcandbondstd_none_p_kernel(tc, x_words, x_scales, w1, gs, offs, 
         y = []
         for t in range(PACK):
             cols = slice(t * P, (t + 1) * P)
-            bank = psum.tile([P, S], F32, name="y_bank%d" % t)
+            bank = bank_tile(t, "y_bank")
             nc.tensor.matmul_mx(bank[:], lhsT=w_codes[:, cols].bitcast(FP8X4), lhsT_scale=w_plane[:, cols],
                                 rhs=x_codes[:].bitcast(FP8X4), rhs_scale=x_plane[:], start=True, stop=True)
             y_t = keep.tile([P, S], F32, name="y%d" % t)
             nc.scalar.copy(y_t[:], bank[:])
             y.append(y_t)
 
-        c_bytes = keep.tile([P, C], U8, name="c_bytes")
-        nc.vector.tensor_copy(c_bytes[:], table_scales[:].indirect(cand_t[:]))
-        c_bytes_dealt = keep.tile([P, C], U8, name="c_bytes_dealt")
-        nc.vector.tensor_copy(c_bytes_dealt[:].rearrange("p (t m) -> p m t", t=PACK), c_bytes[:].rearrange("p (m t) -> p m t", t=PACK))
-        c_plane = place_scale_rows(c_bytes_dealt, "c_plane")
+        c_words = keep.tile([P, C], U32, name="c_words")
+        nc.vector.tensor_copy(c_words[:], table_words[:].indirect(cand_t[:]))
+        c_codes = keep.tile([P, C], U32, name="c_codes", align_bytes=64)
+        nc.vector.tensor_copy(c_codes[:].rearrange("p (t m) -> p m t", t=PACK), c_words[:].rearrange("p (m t) -> p m t", t=PACK))
 
         z_grouped = [keep.tile([P, HALF, PACK], BF16, name="z_grouped%d" % u, align_bytes=64) for u in range(2)]
         pa, pb, dt = {}, {}, {}
 
         def fetch_a(t):
-            pa[t] = keep.tile([P, W], F32, name="pa%d" % t, tag="late" if t == PACK - 1 else "pa%d" % t)
+            pa[t] = keep.tile([P, W], F32, name="pa%d" % t)
             nc.vector.tensor_copy(pa[t][:], y[t][:].indirect(n1_t[:]))
 
         def fetch_b(t):
@@ -123,7 +132,11 @@ def tile_picked_hcandbondstd_none_p_kernel(tc, x_words, x_scales, w1, gs, offs, 
         def put_product(t):
             nc.vector.tensor_tensor(dt[t][:].indirect(n2_t[:]), pa[t][:], pb[t][:], ALU.mult)
             for u in range(2):
-                nc.scalar.activation(z_grouped[u][:, :, t], dt[t][:, u * HALF : (u + 1) * HALF], ACT.Copy, scale=gs_t[:, t : t + 1])
+                src = dt[t][:, u * HALF : (u + 1) * HALF]
+                if t >= 2 and u == 1:
+                    nc.vector.tensor_scalar(z_grouped[u][:, :, t], src, gs_t[:, t : t + 1], None, ALU.mult)
+                else:
+                    nc.scalar.activation(z_grouped[u][:, :, t], src, ACT.Copy, scale=gs_t[:, t : t + 1])
 
         fetch_a(0)
         fetch_b(0)
@@ -135,82 +148,125 @@ def tile_picked_hcandbondstd_none_p_kernel(tc, x_words, x_scales, w1, gs, offs, 
                 fetch_b(t + 1)
             put_product(t)
 
-        c_words = keep.tile([P, C], U32, name="c_words", tag="late")
-        nc.vector.tensor_copy(c_words[:], table_words[:].indirect(cand_t[:]))
-        c_codes = keep.tile([P, C], U32, name="c_codes", align_bytes=64)
-        nc.vector.tensor_copy(c_codes[:].rearrange("p (t m) -> p m t", t=PACK), c_words[:].rearrange("p (m t) -> p m t", t=PACK))
-
         z_codes = keep.tile([P, S], U32, name="z_codes", align_bytes=64)
         z_plane = keep.tile([P, S], U8, name="z_plane", align_bytes=64)
-        for u in range(2):
+        for u in (1, 0):
             cols = slice(u * HALF, (u + 1) * HALF)
             nc.vector.quantize_mx(z_codes[:, cols].bitcast(FP8X4), z_plane[:, cols], z_grouped[u][:].rearrange("p n t -> p (n t)"))
 
-        banks, windows = [], []
-        for t in range(PACK):
-            cols = slice(t * P, (t + 1) * P)
-            bank = psum.tile([P, S], F32, name="s_bank%d" % t)
-            nc.tensor.matmul_mx(bank[:], lhsT=c_codes[:, cols].bitcast(FP8X4), lhsT_scale=c_plane[:, cols],
-                                rhs=z_codes[:].bitcast(FP8X4), rhs_scale=z_plane[:], start=True, stop=True)
-            window = keep.tile([P, S], F32, name="window%d" % t)
-            nc.scalar.copy(window[:], bank[:])
-            banks.append(bank)
-            windows.append(window)
+        def scores(bank, t, cols):
+            rows = slice(t * P, (t + 1) * P)
+            nc.tensor.matmul_mx(bank, lhsT=c_codes[:, rows].bitcast(FP8X4), lhsT_scale=c_plane[:, rows],
+                                rhs=z_codes[:, cols].bitcast(FP8X4), rhs_scale=z_plane[:, cols], start=True, stop=True)
+
+        windows = [keep.tile([P, S], F32, name="window%d" % t) for t in range(PACK)]
+        selfs = [keep.tile([P, S], F32, name="self%d" % t) for t in range(PACK)]
+        rests = [keep.tile([P, S], F32, name="rest%d" % t) for t in range(PACK)]
+        upper, lower = slice(HALF, S), slice(0, HALF)
+        bank_upper = bank_tile(4, "s_upper", HALF)
+        scores(bank_upper[:], 0, upper)
+        bank_lower = bank_tile(3, "s_lower", HALF)
+        scores(bank_lower[:], 0, lower)
+        banks = {}
+        for t in range(1, PACK):
+            banks[t] = bank_tile(4 + t, "s_bank")
+            scores(banks[t][:], t, slice(0, S))
+        nc.vector.tensor_scalar(windows[0][:, upper], bank_upper[:], OWN, None, ALU.mult)
+        nc.scalar.activation(windows[0][:, lower], bank_lower[:], ACT.Copy, scale=OWN)
+        nc.vector.tensor_scalar(selfs[0][:, upper], bank_upper[:], SELF, None, ALU.mult)
+        nc.scalar.activation(selfs[0][:, lower], bank_lower[:], ACT.Copy, scale=SELF)
+        nc.scalar.activation(rests[0][:, upper], bank_upper[:], ACT.Copy, scale=REST)
+        nc.scalar.activation(rests[0][:, lower], bank_lower[:], ACT.Copy, scale=REST)
 
         out_rows = out.rearrange("(p t) n -> t p n", t=PACK)
-        units = [(t, u) for t in range(PACK) for u in range(2)]
+        units = [(t, u) for t in range(PACK) for u in (1, 0)]
+        n_units = len(units)
         st = {}
+
+        def columns(i):
+            return slice(units[i][1] * HALF, (units[i][1] + 1) * HALF)
+
+        def prepare(i):
+            t = i // 2 + 1
+            if t < PACK and i % 2 == 0:
+                nc.scalar.activation(windows[t][:], banks[t][:], ACT.Copy, scale=OWN)
+                nc.scalar.activation(selfs[t][:], banks[t][:], ACT.Copy, scale=SELF)
+            if t < PACK and i % 2 == 1:
+                nc.scalar.activation(rests[t][:], banks[t][:], ACT.Copy, scale=REST)
 
         def gather_first(i):
             t, u = units[i]
-            a = ring.tile([P, HALF], F32, name="a")
-            nc.vector.tensor_copy(a[:], windows[t][:].indirect(n3_t[:, 16 * u : 16 * (u + 1)]))
-            st[i] = {"a": a}
+            first = ring.tile([P, HALF], F32, name="first")
+            nc.vector.tensor_tensor(first[:], windows[t][:].indirect(n3_t[:, 16 * u : 16 * (u + 1)]), selfs[t][:, columns(i)], ALU.subtract)
+            st[i] = {"first": first}
 
         def gather_second(i):
             t, u = units[i]
-            both = ring.tile([P, HALF], F32, name="both")
-            nc.vector.tensor_tensor(both[:], windows[t][:].indirect(n4_t[:, 16 * u : 16 * (u + 1)]), st[i]["a"][:], ALU.add)
-            st[i]["both"] = both
+            num = ring.tile([P, HALF], F32, name="num", bufs=3)
+            nc.vector.tensor_tensor(num[:], windows[t][:].indirect(n4_t[:, 16 * u : 16 * (u + 1)]), st[i]["first"][:], ALU.add)
+            st[i]["num"] = num
+
+        def fold(i):
+            part = ring.tile([P, HALF], F32, name="part")
+            nc.vector.scalar_tensor_tensor(part[:], st[i]["first"][:], 2.0, st[i]["num"][:], ALU.mult, ALU.subtract)
+            st[i]["part"] = part
+
+        def turn_and_add(dst, terms):
+            for b in range(HALF // P):
+                block = slice(b * P, (b + 1) * P)
+                for n, term in enumerate(terms):
+                    nc.tensor.matmul(dst[:, block], lhsT=term[:, block], rhs=ident[:], is_transpose=True,
+                                     start=(n == 0), stop=(n == len(terms) - 1))
+
+        def squares(i, mean, diff):
+            mean2 = ring.tile([P, HALF], F32, name="mean2")
+            nc.scalar.activation(mean2[:], mean, ACT.Square, scale=math.sqrt(0.5) * 1.2)
+            diff2 = ring.tile([P, HALF], F32, name="diff2")
+            nc.scalar.activation(diff2[:], diff, ACT.Square, scale=math.sqrt(0.5) * 3.2)
+            st[i]["mean2"], st[i]["diff2"] = mean2, diff2
 
         def linear(i):
-            t, u = units[i]
-            own = banks[t][:, u * HALF : (u + 1) * HALF]
-            both = st[i]["both"]
-            diff = ring.tile([P, HALF], F32, name="diff")
-            nc.vector.scalar_tensor_tensor(diff[:], both[:], -0.5, st[i]["a"][:], ALU.mult, ALU.add)
-            mean = ring.tile([P, HALF], F32, name="mean")
-            nc.vector.scalar_tensor_tensor(mean[:], both[:], 0.6, own, ALU.mult, ALU.subtract)
-            num = ring.tile([P, HALF], F32, name="num")
-            nc.vector.scalar_tensor_tensor(num[:], both[:], -0.3125 / 0.6875, own, ALU.mult, ALU.add)
-            diff2 = ring.tile([P, HALF], F32, name="diff2")
-            nc.scalar.activation(diff2[:], diff[:], ACT.Square, scale=math.sqrt(0.5) / 8)
-            mean2 = ring.tile([P, HALF], F32, name="mean2")
-            nc.scalar.activation(mean2[:], mean[:], ACT.Square, scale=math.sqrt(0.5) * 0.625 / 16)
-            st[i]["num"], st[i]["diff2"], st[i]["mean2"] = num, diff2, mean2
+            t = units[i][0]
+            if i < n_units - 1:
+                both = bank_tile(i % 2, "both")
+                turn_and_add(both[:, lower], (st[i]["num"][:], rests[t][:, columns(i)]))
+                turn_and_add(both[:, upper], (st[i]["part"][:], selfs[t][:, columns(i)]))
+                squares(i, both[:, lower], both[:, upper])
+            else:
+                mean = ring.tile([P, HALF], F32, name="mean")
+                nc.vector.tensor_tensor(mean[:], st[i]["num"][:], rests[t][:, columns(i)], ALU.add)
+                diff = ring.tile([P, HALF], F32, name="diff")
+                nc.vector.tensor_tensor(diff[:], st[i]["part"][:], selfs[t][:, columns(i)], ALU.add)
+                squares(i, mean[:], diff[:])
 
         def spread(i):
-            den = ring.tile([P, HALF], F32, name="den")
-            nc.vector.tensor_tensor(den[:], st[i]["diff2"][:], st[i]["mean2"][:], ALU.add)
             inv = ring.tile([P, HALF], F32, name="inv")
+            if i < n_units - 1:
+                den = bank_tile(2 + i % 2, "den", HALF)
+                turn_and_add(den[:], (st[i]["mean2"][:], st[i]["diff2"][:]))
+            else:
+                den = ring.tile([P, HALF], F32, name="den_sum")
+                nc.vector.tensor_tensor(den[:], st[i]["mean2"][:], st[i]["diff2"][:], ALU.add)
             nc.scalar.activation(inv[:], den[:], ACT.Abs_reciprocal_sqrt, bias=0.25)
             st[i]["inv"] = inv
 
         def finish(i):
-            t, u = units[i]
             res = ring.tile([P, HALF], F32, name="res")
-            nc.vector.scalar_tensor_tensor(res[:], st[i]["num"][:], 0.6875 / 16, st[i]["inv"][:], ALU.mult, ALU.mult)
-            nc.sync.dma_start(out_rows[t][:, u * HALF : (u + 1) * HALF], res[:])
+            nc.vector.tensor_tensor(res[:], st[i]["num"][:], st[i]["inv"][:], ALU.mult)
+            nc.sync.dma_start(out_rows[units[i][0]][:, columns(i)], res[:])
 
-        n = len(units)
-        for i in range(n + 2):
-            if i < n:
+        for i in range(n_units + 3):
+            if i < n_units:
                 gather_first(i)
-            if 0 <= i - 2 < n:
-                spread(i - 2)
-            if i < n:
+            if 0 <= i - 1 < n_units:
+                fold(i - 1)
+            if 0 <= i - 3 < n_units:
+                finish(i - 3)
+            if i < n_units:
                 gather_second(i)
-            if 0 <= i - 1 < n:
+            if 0 <= i - 2 < n_units:
+                spread(i - 2)
+            if 0 <= i - 1 < n_units:
                 linear(i - 1)
-            if 0 <= i - 2 < n:
-                finish(i - 2)
+            if i < n_units:
+                prepare(i)

@@ -67,26 +67,29 @@ def tile_picked_hcandbondstd_none_p_kernel(tc, x_words, x_scales, w1, gs, offs, 
         n3_t = load_list(n3, "n3_t")
         n4_t = load_list(n4, "n4_t")
         gs_t = keep.tile([P, PACK], F32, name="gs_t")
-        nc.gpsimd.dma_start(gs_t[:], gs.rearrange("(p t) o -> p (t o)", t=PACK))
+        nc.sync.dma_start(gs_t[:], gs.rearrange("(p t) o -> p (t o)", t=PACK))
         ident = keep.tile([P, P], F32, name="ident")
         make_identity(nc, ident[:])
 
-        def place_scale_rows(src, name):
+        def place_scale_rows(src, name, queue):
             plane = keep.tile([P, S], U8, name=name, align_bytes=64)
             nc.vector.tensor_copy(plane[:].bitcast(I32), src[:].bitcast(I32))
             for e in range(2):
-                nc.sync.dma_start(plane[2 + e : P : 32, :].bitcast(I32), src[16 + e : P : 32, :].bitcast(I32))
+                queue.dma_start(plane[2 + e : P : 32, :].bitcast(I32), src[16 + e : P : 32, :].bitcast(I32))
             return plane
 
         x_bytes = keep.tile([P, S], U8, name="x_bytes")
         nc.vector.tensor_copy(x_bytes[:], table_scales[:].indirect(offs_t[:]))
-        x_plane = place_scale_rows(x_bytes, "x_plane")
+        x_plane = place_scale_rows(x_bytes, "x_plane", nc.sync)
 
         c_bytes = keep.tile([P, C], U8, name="c_bytes")
         nc.vector.tensor_copy(c_bytes[:], table_scales[:].indirect(cand_t[:]))
         c_bytes_dealt = keep.tile([P, C], U8, name="c_bytes_dealt")
         nc.vector.tensor_copy(c_bytes_dealt[:].rearrange("p (t m) -> p t m", t=PACK), c_bytes[:].rearrange("p (m t) -> p t m", t=PACK))
-        c_plane = place_scale_rows(c_bytes_dealt, "c_plane")
+        c_plane = keep.tile([P, C], U8, name="c_plane", align_bytes=64)
+        nc.gpsimd.memset(c_plane[:].bitcast(I32), 0)
+        for row in range(4):
+            nc.sync.dma_start(c_plane[row:P:32, :].bitcast(I32), c_bytes_dealt[16 * (row // 2) + row % 2 : P : 32, :].bitcast(I32))
 
         w_grouped = keep.tile([P, PACK, P, PACK], BF16, name="w_grouped", align_bytes=64)
         for n, (lo, hi) in enumerate(W_PIECES):
@@ -99,26 +102,27 @@ def tile_picked_hcandbondstd_none_p_kernel(tc, x_words, x_scales, w1, gs, offs, 
         x_codes = keep.tile([P, S], U32, name="x_codes", align_bytes=64)
         nc.vector.tensor_copy(x_codes[:], table_words[:].indirect(offs_t[:]))
 
-        y = []
+        upper, lower = slice(HALF, S), slice(0, HALF)
+
+        def project(bank, t, cols):
+            rows = slice(t * P, (t + 1) * P)
+            nc.tensor.matmul_mx(bank, lhsT=w_codes[:, rows].bitcast(FP8X4), lhsT_scale=w_plane[:, rows],
+                                rhs=x_codes[:, cols].bitcast(FP8X4), rhs_scale=x_plane[:, cols], start=True, stop=True)
+
+        y = [keep.tile([P, S], F32, name="y%d" % t) for t in range(PACK)]
         for t in range(PACK):
-            cols = slice(t * P, (t + 1) * P)
             bank = bank_tile(t, "y_bank")
-            nc.tensor.matmul_mx(bank[:], lhsT=w_codes[:, cols].bitcast(FP8X4), lhsT_scale=w_plane[:, cols],
-                                rhs=x_codes[:].bitcast(FP8X4), rhs_scale=x_plane[:], start=True, stop=True)
-            y_t = keep.tile([P, S], F32, name="y%d" % t)
-            nc.scalar.copy(y_t[:], bank[:])
-            y.append(y_t)
+            project(bank[:], t, slice(0, S))
+            nc.scalar.copy(y[t][:], bank[:])
 
         c_words = keep.tile([P, C], U32, name="c_words")
         nc.vector.tensor_copy(c_words[:], table_words[:].indirect(cand_t[:]))
-        c_codes = keep.tile([P, C], U32, name="c_codes", align_bytes=64)
-        nc.vector.tensor_copy(c_codes[:].rearrange("p (t m) -> p m t", t=PACK), c_words[:].rearrange("p (m t) -> p m t", t=PACK))
 
         z_grouped = [keep.tile([P, HALF, PACK], BF16, name="z_grouped%d" % u, align_bytes=64) for u in range(2)]
         pa, pb, dt = {}, {}, {}
 
         def fetch_a(t):
-            pa[t] = keep.tile([P, W], F32, name="pa%d" % t)
+            pa[t] = keep.tile([P, W], F32, name="pa%d" % t, tag="late" if t == PACK - 1 else "pa%d" % t, align_bytes=64)
             nc.vector.tensor_copy(pa[t][:], y[t][:].indirect(n1_t[:]))
 
         def fetch_b(t):
@@ -131,7 +135,9 @@ def tile_picked_hcandbondstd_none_p_kernel(tc, x_words, x_scales, w1, gs, offs, 
 
         def put_product(t):
             nc.vector.tensor_tensor(dt[t][:].indirect(n2_t[:]), pa[t][:], pb[t][:], ALU.mult)
-            for u in range(2):
+
+        def weigh(t):
+            for u in (1, 0):
                 src = dt[t][:, u * HALF : (u + 1) * HALF]
                 if t >= 2 and u == 1:
                     nc.vector.tensor_scalar(z_grouped[u][:, :, t], src, gs_t[:, t : t + 1], None, ALU.mult)
@@ -146,7 +152,14 @@ def tile_picked_hcandbondstd_none_p_kernel(tc, x_words, x_scales, w1, gs, offs, 
             put_sum(t)
             if t + 1 < PACK:
                 fetch_b(t + 1)
+            else:
+                weigh(t - 1)
             put_product(t)
+            if t != PACK - 2:
+                weigh(t)
+
+        c_codes = keep.tile([P, C], U32, name="c_codes", tag="late", align_bytes=64)
+        nc.vector.tensor_copy(c_codes[:].rearrange("p (t m) -> p m t", t=PACK), c_words[:].rearrange("p (m t) -> p m t", t=PACK))
 
         z_codes = keep.tile([P, S], U32, name="z_codes", align_bytes=64)
         z_plane = keep.tile([P, S], U8, name="z_plane", align_bytes=64)
@@ -162,7 +175,6 @@ def tile_picked_hcandbondstd_none_p_kernel(tc, x_words, x_scales, w1, gs, offs, 
         windows = [keep.tile([P, S], F32, name="window%d" % t) for t in range(PACK)]
         selfs = [keep.tile([P, S], F32, name="self%d" % t) for t in range(PACK)]
         rests = [keep.tile([P, S], F32, name="rest%d" % t) for t in range(PACK)]
-        upper, lower = slice(HALF, S), slice(0, HALF)
         bank_upper = bank_tile(4, "s_upper", HALF)
         scores(bank_upper[:], 0, upper)
         bank_lower = bank_tile(3, "s_lower", HALF)
@@ -178,95 +190,70 @@ def tile_picked_hcandbondstd_none_p_kernel(tc, x_words, x_scales, w1, gs, offs, 
         nc.scalar.activation(rests[0][:, upper], bank_upper[:], ACT.Copy, scale=REST)
         nc.scalar.activation(rests[0][:, lower], bank_lower[:], ACT.Copy, scale=REST)
 
+        for t in range(1, PACK):
+            for tiles, scale in ((windows, OWN), (selfs, SELF), (rests, REST)):
+                nc.scalar.activation(tiles[t][:], banks[t][:], ACT.Copy, scale=scale)
+
         out_rows = out.rearrange("(p t) n -> t p n", t=PACK)
-        units = [(t, u) for t in range(PACK) for u in (1, 0)]
-        n_units = len(units)
-        st = {}
+        firsts = [keep.tile([P, S], F32, name="first%d" % t) for t in range(PACK)]
+        parts = [keep.tile([P, S], F32, name="part%d" % t) for t in range(PACK)]
+        nums = {}
 
-        def columns(i):
-            return slice(units[i][1] * HALF, (units[i][1] + 1) * HALF)
+        def offsets(tile, cols):
+            return tile[:, cols.start // 16 : cols.stop // 16]
 
-        def prepare(i):
-            t = i // 2 + 1
-            if t < PACK and i % 2 == 0:
-                nc.scalar.activation(windows[t][:], banks[t][:], ACT.Copy, scale=OWN)
-                nc.scalar.activation(selfs[t][:], banks[t][:], ACT.Copy, scale=SELF)
-            if t < PACK and i % 2 == 1:
-                nc.scalar.activation(rests[t][:], banks[t][:], ACT.Copy, scale=REST)
+        def look_up(t):
+            nums[t] = ring.tile([P, S], F32, name="num", bufs=3)
+            for cols in (upper, lower):
+                nc.vector.tensor_tensor(firsts[t][:, cols], windows[t][:].indirect(offsets(n3_t, cols)), selfs[t][:, cols], ALU.subtract)
+            for cols in (upper, lower):
+                nc.vector.tensor_tensor(nums[t][:, cols], windows[t][:].indirect(offsets(n4_t, cols)), firsts[t][:, cols], ALU.add)
+            for cols in (upper, lower):
+                nc.vector.scalar_tensor_tensor(parts[t][:, cols], firsts[t][:, cols], 2.0, nums[t][:, cols], ALU.mult, ALU.subtract)
 
-        def gather_first(i):
-            t, u = units[i]
-            first = ring.tile([P, HALF], F32, name="first")
-            nc.vector.tensor_tensor(first[:], windows[t][:].indirect(n3_t[:, 16 * u : 16 * (u + 1)]), selfs[t][:, columns(i)], ALU.subtract)
-            st[i] = {"first": first}
+        units = [(t, slice(0, S)) for t in range(PACK - 1)] + [(PACK - 1, upper), (PACK - 1, lower)]
+        last = len(units) - 1
+        invs = {}
 
-        def gather_second(i):
-            t, u = units[i]
-            num = ring.tile([P, HALF], F32, name="num", bufs=3)
-            nc.vector.tensor_tensor(num[:], windows[t][:].indirect(n4_t[:, 16 * u : 16 * (u + 1)]), st[i]["first"][:], ALU.add)
-            st[i]["num"] = num
-
-        def fold(i):
-            part = ring.tile([P, HALF], F32, name="part")
-            nc.vector.scalar_tensor_tensor(part[:], st[i]["first"][:], 2.0, st[i]["num"][:], ALU.mult, ALU.subtract)
-            st[i]["part"] = part
-
-        def turn_and_add(dst, terms):
-            for b in range(HALF // P):
+        def add_pair(i, name, bank, left, right):
+            width = left.shape[1]
+            if i == last:
+                total = ring.tile([P, width], F32, name=name)
+                nc.vector.tensor_tensor(total[:], left, right, ALU.add)
+                return total[:]
+            total = bank_tile(bank, name, width)
+            for b in range(width // P):
                 block = slice(b * P, (b + 1) * P)
-                for n, term in enumerate(terms):
-                    nc.tensor.matmul(dst[:, block], lhsT=term[:, block], rhs=ident[:], is_transpose=True,
-                                     start=(n == 0), stop=(n == len(terms) - 1))
-
-        def squares(i, mean, diff):
-            mean2 = ring.tile([P, HALF], F32, name="mean2")
-            nc.scalar.activation(mean2[:], mean, ACT.Square, scale=math.sqrt(0.5) * 1.2)
-            diff2 = ring.tile([P, HALF], F32, name="diff2")
-            nc.scalar.activation(diff2[:], diff, ACT.Square, scale=math.sqrt(0.5) * 3.2)
-            st[i]["mean2"], st[i]["diff2"] = mean2, diff2
-
-        def linear(i):
-            t = units[i][0]
-            if i < n_units - 1:
-                both = bank_tile(i % 2, "both")
-                turn_and_add(both[:, lower], (st[i]["num"][:], rests[t][:, columns(i)]))
-                turn_and_add(both[:, upper], (st[i]["part"][:], selfs[t][:, columns(i)]))
-                squares(i, both[:, lower], both[:, upper])
-            else:
-                mean = ring.tile([P, HALF], F32, name="mean")
-                nc.vector.tensor_tensor(mean[:], st[i]["num"][:], rests[t][:, columns(i)], ALU.add)
-                diff = ring.tile([P, HALF], F32, name="diff")
-                nc.vector.tensor_tensor(diff[:], st[i]["part"][:], selfs[t][:, columns(i)], ALU.add)
-                squares(i, mean[:], diff[:])
+                nc.tensor.matmul(total[:, block], lhsT=left[:, block], rhs=ident[:], is_transpose=True, start=True, stop=False)
+                nc.tensor.matmul(total[:, block], lhsT=right[:, block], rhs=ident[:], is_transpose=True, start=False, stop=True)
+            return total[:]
 
         def spread(i):
-            inv = ring.tile([P, HALF], F32, name="inv")
-            if i < n_units - 1:
-                den = bank_tile(2 + i % 2, "den", HALF)
-                turn_and_add(den[:], (st[i]["mean2"][:], st[i]["diff2"][:]))
-            else:
-                den = ring.tile([P, HALF], F32, name="den_sum")
-                nc.vector.tensor_tensor(den[:], st[i]["mean2"][:], st[i]["diff2"][:], ALU.add)
-            nc.scalar.activation(inv[:], den[:], ACT.Abs_reciprocal_sqrt, bias=0.25)
-            st[i]["inv"] = inv
+            t, cols = units[i]
+            width = cols.stop - cols.start
+            first_bank = 3 * (i % 2)
+            mean = add_pair(i, "mean", first_bank, nums[t][:, cols], rests[t][:, cols])
+            mean2 = ring.tile([P, width], F32, name="mean2")
+            nc.scalar.activation(mean2[:], mean, ACT.Square, scale=math.sqrt(0.5) * 1.2)
+            diff = add_pair(i, "diff", first_bank + 1, parts[t][:, cols], selfs[t][:, cols])
+            diff2 = ring.tile([P, width], F32, name="diff2")
+            nc.scalar.activation(diff2[:], diff, ACT.Square, scale=math.sqrt(0.5) * 3.2)
+            den = add_pair(i, "den", first_bank + 2, mean2[:], diff2[:])
+            invs[i] = ring.tile([P, width], F32, name="inv")
+            nc.scalar.activation(invs[i][:], den, ACT.Abs_reciprocal_sqrt, bias=0.25)
 
         def finish(i):
-            res = ring.tile([P, HALF], F32, name="res")
-            nc.vector.tensor_tensor(res[:], st[i]["num"][:], st[i]["inv"][:], ALU.mult)
-            nc.sync.dma_start(out_rows[units[i][0]][:, columns(i)], res[:])
+            t, cols = units[i]
+            res = ring.tile([P, cols.stop - cols.start], F32, name="res")
+            nc.vector.tensor_tensor(res[:], nums[t][:, cols], invs[i][:], ALU.mult)
+            nc.sync.dma_start(out_rows[t][:, cols], res[:])
 
-        for i in range(n_units + 3):
-            if i < n_units:
-                gather_first(i)
-            if 0 <= i - 1 < n_units:
-                fold(i - 1)
-            if 0 <= i - 3 < n_units:
-                finish(i - 3)
-            if i < n_units:
-                gather_second(i)
-            if 0 <= i - 2 < n_units:
-                spread(i - 2)
-            if 0 <= i - 1 < n_units:
-                linear(i - 1)
-            if i < n_units:
-                prepare(i)
+        for t in range(PACK):
+            if t >= 3:
+                finish(t - 3)
+            look_up(t)
+            spread(t)
+        finish(1)
+        spread(last)
+        for i in range(2, len(units)):
+            finish(i)

@@ -24,6 +24,8 @@ W_PIECES = ((0, 128), (128, 256), (256, 512))
 OWN = -0.3125 / 16
 SELF = 2.2 * OWN
 REST = 8 / 15 * OWN
+MEAN = math.sqrt(0.5) * 1.2
+DIFF = math.sqrt(0.5) * 3.2
 
 
 def tile_picked_hcandbondstd_none_p_kernel(tc, x_words, x_scales, w1, gs, offs, n1, n2, cand, n3, n4, out):
@@ -174,7 +176,7 @@ def tile_picked_hcandbondstd_none_p_kernel(tc, x_words, x_scales, w1, gs, offs, 
 
         windows = [keep.tile([P, S], F32, name="window%d" % t) for t in range(PACK)]
         selfs = [keep.tile([P, S], F32, name="self%d" % t) for t in range(PACK)]
-        rests = [keep.tile([P, S], F32, name="rest%d" % t) for t in range(PACK)]
+        rests = {0: keep.tile([P, S], F32, name="rest0")}
         bank_upper = bank_tile(4, "s_upper", HALF)
         scores(bank_upper[:], 0, upper)
         bank_lower = bank_tile(3, "s_lower", HALF)
@@ -191,7 +193,7 @@ def tile_picked_hcandbondstd_none_p_kernel(tc, x_words, x_scales, w1, gs, offs, 
         nc.scalar.activation(rests[0][:, lower], bank_lower[:], ACT.Copy, scale=REST)
 
         for t in range(1, PACK):
-            for tiles, scale in ((windows, OWN), (selfs, SELF), (rests, REST)):
+            for tiles, scale in ((windows, OWN), (selfs, SELF)):
                 nc.scalar.activation(tiles[t][:], banks[t][:], ACT.Copy, scale=scale)
 
         out_rows = out.rearrange("(p t) n -> t p n", t=PACK)
@@ -211,49 +213,62 @@ def tile_picked_hcandbondstd_none_p_kernel(tc, x_words, x_scales, w1, gs, offs, 
             for cols in (upper, lower):
                 nc.vector.scalar_tensor_tensor(parts[t][:, cols], firsts[t][:, cols], 2.0, nums[t][:, cols], ALU.mult, ALU.subtract)
 
-        units = [(t, slice(0, S)) for t in range(PACK - 1)] + [(PACK - 1, upper), (PACK - 1, lower)]
-        last = len(units) - 1
         invs = {}
+        whole = slice(0, S)
 
-        def add_pair(i, name, bank, left, right):
-            width = left.shape[1]
-            if i == last:
-                total = ring.tile([P, width], F32, name=name)
-                nc.vector.tensor_tensor(total[:], left, right, ALU.add)
-                return total[:]
-            total = bank_tile(bank, name, width)
-            for b in range(width // P):
+        def turn_and_add(total, left, right, blocks):
+            for b in blocks:
                 block = slice(b * P, (b + 1) * P)
-                nc.tensor.matmul(total[:, block], lhsT=left[:, block], rhs=ident[:], is_transpose=True, start=True, stop=False)
-                nc.tensor.matmul(total[:, block], lhsT=right[:, block], rhs=ident[:], is_transpose=True, start=False, stop=True)
-            return total[:]
+                place = slice(b * P % total.shape[1], b * P % total.shape[1] + P)
+                nc.tensor.matmul(total[:, place], lhsT=left[:, block], rhs=ident[:], is_transpose=True, start=True, stop=False)
+                nc.tensor.matmul(total[:, place], lhsT=right[:, block], rhs=ident[:], is_transpose=True, start=False, stop=True)
 
-        def spread(i):
-            t, cols = units[i]
-            width = cols.stop - cols.start
-            first_bank = 3 * (i % 2)
-            mean = add_pair(i, "mean", first_bank, nums[t][:, cols], rests[t][:, cols])
-            mean2 = ring.tile([P, width], F32, name="mean2")
-            nc.scalar.activation(mean2[:], mean, ACT.Square, scale=math.sqrt(0.5) * 1.2)
-            diff = add_pair(i, "diff", first_bank + 1, parts[t][:, cols], selfs[t][:, cols])
-            diff2 = ring.tile([P, width], F32, name="diff2")
-            nc.scalar.activation(diff2[:], diff, ACT.Square, scale=math.sqrt(0.5) * 3.2)
-            den = add_pair(i, "den", first_bank + 2, mean2[:], diff2[:])
-            invs[i] = ring.tile([P, width], F32, name="inv")
-            nc.scalar.activation(invs[i][:], den, ACT.Abs_reciprocal_sqrt, bias=0.25)
+        def spread_on_tensor(t):
+            mean = bank_tile(0, "mean")
+            turn_and_add(mean, nums[t], rests[t], (2, 3, 0, 1))
+            mean2 = ring.tile([P, S], F32, name="mean2", bufs=1)
+            nc.scalar.activation(mean2[:], mean[:], ACT.Square, scale=MEAN)
+            diff2 = ring.tile([P, S], F32, name="diff2", bufs=1)
+            for u, cols in ((1, upper), (0, lower)):
+                diff = bank_tile(1 + u, "diff", HALF)
+                turn_and_add(diff, parts[t], selfs[t], (2 * u, 2 * u + 1))
+                nc.scalar.activation(diff2[:, cols], diff[:], ACT.Square, scale=DIFF)
+            if t + 1 < PACK - 1:
+                rests[t + 1] = keep.tile([P, S], F32, name="rest%d" % (t + 1), tag="part%d" % t)
+                nc.scalar.activation(rests[t + 1][:], banks[t + 1][:], ACT.Copy, scale=REST)
+            den = bank_tile(3, "den")
+            turn_and_add(den, mean2, diff2, (2, 3, 0, 1))
+            invs[t] = ring.tile([P, S], F32, name="inv")
+            nc.scalar.activation(invs[t][:], den[:], ACT.Abs_reciprocal_sqrt, bias=0.25)
 
-        def finish(i):
-            t, cols = units[i]
+        def spread_on_vector(t):
+            mean = keep.tile([P, S], F32, name="mean_last")
+            nc.vector.scalar_tensor_tensor(mean[:], windows[t][:], 8 / 15, nums[t][:], ALU.mult, ALU.add)
+            mean2 = ring.tile([P, S], F32, name="mean2", bufs=1)
+            nc.scalar.activation(mean2[:], mean[:], ACT.Square, scale=MEAN)
+            diff = keep.tile([P, S], F32, name="diff_last")
+            diff2 = ring.tile([P, S], F32, name="diff2", bufs=1)
+            for cols in (upper, lower):
+                nc.vector.tensor_tensor(diff[:, cols], parts[t][:, cols], selfs[t][:, cols], ALU.add)
+                nc.scalar.activation(diff2[:, cols], diff[:, cols], ACT.Square, scale=DIFF)
+            finish(t - 2, whole)
+            den = keep.tile([P, S], F32, name="den_last")
+            invs[t] = ring.tile([P, S], F32, name="inv")
+            for cols in (upper, lower):
+                nc.vector.tensor_tensor(den[:, cols], mean2[:, cols], diff2[:, cols], ALU.add)
+                nc.scalar.activation(invs[t][:, cols], den[:, cols], ACT.Abs_reciprocal_sqrt, bias=0.25)
+
+        def finish(t, cols):
             res = ring.tile([P, cols.stop - cols.start], F32, name="res")
-            nc.vector.tensor_tensor(res[:], nums[t][:, cols], invs[i][:], ALU.mult)
+            nc.vector.tensor_tensor(res[:], nums[t][:, cols], invs[t][:, cols], ALU.mult)
             nc.sync.dma_start(out_rows[t][:, cols], res[:])
 
-        for t in range(PACK):
-            if t >= 3:
-                finish(t - 3)
+        for t in range(PACK - 1):
             look_up(t)
-            spread(t)
-        finish(1)
-        spread(last)
-        for i in range(2, len(units)):
-            finish(i)
+            spread_on_tensor(t)
+        finish(0, whole)
+        look_up(PACK - 1)
+        spread_on_vector(PACK - 1)
+        finish(PACK - 2, whole)
+        finish(PACK - 1, upper)
+        finish(PACK - 1, lower)

@@ -19,13 +19,18 @@ ACT = mybir.ActivationFunctionType
 
 P = 128
 PACK = 4
-HALF = 256
+GROUP = 16
+QUADRANT = 32
+HALF = S // 2
+LOWER, UPPER, WHOLE = slice(0, HALF), slice(HALF, S), slice(0, S)
+PAIR_ORDER = (2, 0, 1, 3)
 W_PIECES = ((0, 128), (128, 256), (256, 512))
-OWN = -0.3125 / 16
-SELF = 2.2 * OWN
-REST = 8 / 15 * OWN
-MEAN = math.sqrt(0.5) * 1.2
-DIFF = math.sqrt(0.5) * 3.2
+WINDOW_SCALE = -0.3125 * 0.0625
+OWN_SCALE = 2.2 * WINDOW_SCALE
+REST_SHARE = 8 / 15
+MEAN_SCALE = math.sqrt(0.5) * 1.2
+DIFF_SCALE = math.sqrt(0.5) * 3.2
+MEAN_BANK, DIFF_BANK, DEN_BANK = 0, 1, 3
 
 
 def tile_picked_hcandbondstd_none_p_kernel(tc, x_words, x_scales, w1, gs, offs, n1, n2, cand, n3, n4, out):
@@ -40,15 +45,23 @@ def tile_picked_hcandbondstd_none_p_kernel(tc, x_words, x_scales, w1, gs, offs, 
             nc.sync.dma_start(tile[:], dram)
             return tile
 
+        def offsets(tile, cols):
+            return tile[:, cols.start // GROUP : cols.stop // GROUP]
+
         def bank_tile(b, name, width=S):
             return psum.tile([P, width], F32, name=name, tag="bank%d" % b)
+
+        def product(bank, lhs_codes, lhs_scales, t, rhs_codes, rhs_scales, cols):
+            rows = slice(t * P, (t + 1) * P)
+            nc.tensor.matmul_mx(bank[:], lhsT=lhs_codes[:, rows].bitcast(FP8X4), lhsT_scale=lhs_scales[:, rows],
+                                rhs=rhs_codes[:, cols].bitcast(FP8X4), rhs_scale=rhs_scales[:, cols], start=True, stop=True)
 
         table_scales = keep.tile([P, T], U8, name="table_scales")
         nc.gpsimd.memset(table_scales[:].bitcast(I32), 0)
         one = keep.tile([P, 1], F32, name="one")
         nc.vector.memset(one[:], 1.0)
-        warm = keep.tile([P, 1], F32, name="warm")
-        nc.scalar.activation(warm[:], one[:], ACT.Abs_reciprocal_sqrt)
+        preload = keep.tile([P, 1], F32, name="preload")
+        nc.scalar.activation(preload[:], one[:], ACT.Abs_reciprocal_sqrt)
 
         offs_t = load_list(offs, "offs_t")
         cand_t = load_list(cand, "cand_t")
@@ -61,7 +74,7 @@ def tile_picked_hcandbondstd_none_p_kernel(tc, x_words, x_scales, w1, gs, offs, 
             if n == 0:
                 scale_rows = x_scales[0].rearrange("(r e) n -> e r n", e=2)
                 for e in range(2):
-                    nc.sync.dma_start(table_scales[e:P:16, :].bitcast(I32), scale_rows[e].bitcast(I32))
+                    nc.sync.dma_start(table_scales[e:P:GROUP, :].bitcast(I32), scale_rows[e].bitcast(I32))
         table_words = keep.tile([P, T], U32, name="table_words")
         nc.sync.dma_start(table_words[:].bitcast(I32), x_words[0].rearrange("p n t -> p (n t)").bitcast(I32))
         n1_t = load_list(n1, "n1_t")
@@ -73,48 +86,46 @@ def tile_picked_hcandbondstd_none_p_kernel(tc, x_words, x_scales, w1, gs, offs, 
         ident = keep.tile([P, P], F32, name="ident")
         make_identity(nc, ident[:])
 
-        def place_scale_rows(src, name, queue):
-            plane = keep.tile([P, S], U8, name=name, align_bytes=64)
-            nc.vector.tensor_copy(plane[:].bitcast(I32), src[:].bitcast(I32))
-            for e in range(2):
-                queue.dma_start(plane[2 + e : P : 32, :].bitcast(I32), src[16 + e : P : 32, :].bitcast(I32))
-            return plane
+        def move_scale_row(dst, src, row):
+            gathered_at = GROUP * (row // 2) + row % 2
+            nc.sync.dma_start(dst[row:P:QUADRANT, :].bitcast(I32), src[gathered_at:P:QUADRANT, :].bitcast(I32))
 
         x_bytes = keep.tile([P, S], U8, name="x_bytes")
         nc.vector.tensor_copy(x_bytes[:], table_scales[:].indirect(offs_t[:]))
-        x_plane = place_scale_rows(x_bytes, "x_plane", nc.sync)
+        x_scale = keep.tile([P, S], U8, name="x_scale", align_bytes=64)
+        nc.vector.tensor_copy(x_scale[:].bitcast(I32), x_bytes[:].bitcast(I32))
+        for row in (2, 3):
+            move_scale_row(x_scale, x_bytes, row)
 
         c_bytes = keep.tile([P, C], U8, name="c_bytes")
         nc.vector.tensor_copy(c_bytes[:], table_scales[:].indirect(cand_t[:]))
         c_bytes_dealt = keep.tile([P, C], U8, name="c_bytes_dealt")
         nc.vector.tensor_copy(c_bytes_dealt[:].rearrange("p (t m) -> p t m", t=PACK), c_bytes[:].rearrange("p (m t) -> p t m", t=PACK))
-        c_plane = keep.tile([P, C], U8, name="c_plane", align_bytes=64)
-        nc.gpsimd.memset(c_plane[:].bitcast(I32), 0)
+        c_scale = keep.tile([P, C], U8, name="c_scale", align_bytes=64)
+        nc.gpsimd.memset(c_scale[:].bitcast(I32), 0)
         for row in range(4):
-            nc.sync.dma_start(c_plane[row:P:32, :].bitcast(I32), c_bytes_dealt[16 * (row // 2) + row % 2 : P : 32, :].bitcast(I32))
+            move_scale_row(c_scale, c_bytes_dealt, row)
 
         w_grouped = keep.tile([P, PACK, P, PACK], BF16, name="w_grouped", align_bytes=64)
         for n, (lo, hi) in enumerate(W_PIECES):
             nc.scalar.copy(w_grouped[:, :, lo // PACK : hi // PACK, :].rearrange("p t m j -> p m t j"),
                            w_raw[n][:].rearrange("p j (m t) -> p m t j", t=PACK))
         w_codes = keep.tile([P, H], U32, name="w_codes", align_bytes=64)
-        w_plane = keep.tile([P, H], U8, name="w_plane", align_bytes=64)
-        nc.vector.quantize_mx(w_codes[:].bitcast(FP8X4), w_plane[:], w_grouped[:].rearrange("p t m j -> p (t m j)"))
+        w_scale = keep.tile([P, H], U8, name="w_scale", align_bytes=64)
+        nc.vector.quantize_mx(w_codes[:].bitcast(FP8X4), w_scale[:], w_grouped[:].rearrange("p t m j -> p (t m j)"))
 
         x_codes = keep.tile([P, S], U32, name="x_codes", align_bytes=64)
-        nc.vector.tensor_copy(x_codes[:], table_words[:].indirect(offs_t[:]))
-
-        upper, lower = slice(HALF, S), slice(0, HALF)
-
-        def project(bank, t, cols):
-            rows = slice(t * P, (t + 1) * P)
-            nc.tensor.matmul_mx(bank, lhsT=w_codes[:, rows].bitcast(FP8X4), lhsT_scale=w_plane[:, rows],
-                                rhs=x_codes[:, cols].bitcast(FP8X4), rhs_scale=x_plane[:, cols], start=True, stop=True)
+        for cols in (LOWER, UPPER):
+            nc.vector.tensor_copy(x_codes[:, cols], table_words[:].indirect(offsets(offs_t, cols)))
 
         y = [keep.tile([P, S], F32, name="y%d" % t) for t in range(PACK)]
-        for t in range(PACK):
+        for b, cols in ((PAIR_ORDER[0], LOWER), (PACK, UPPER)):
+            bank = bank_tile(b, "y_half", HALF)
+            product(bank, w_codes, w_scale, PAIR_ORDER[0], x_codes, x_scale, cols)
+            nc.scalar.copy(y[PAIR_ORDER[0]][:, cols], bank[:])
+        for t in PAIR_ORDER[1:]:
             bank = bank_tile(t, "y_bank")
-            project(bank[:], t, slice(0, S))
+            product(bank, w_codes, w_scale, t, x_codes, x_scale, WHOLE)
             nc.scalar.copy(y[t][:], bank[:])
 
         c_words = keep.tile([P, C], U32, name="c_words")
@@ -122,9 +133,10 @@ def tile_picked_hcandbondstd_none_p_kernel(tc, x_words, x_scales, w1, gs, offs, 
 
         z_grouped = [keep.tile([P, HALF, PACK], BF16, name="z_grouped%d" % u, align_bytes=64) for u in range(2)]
         pa, pb, dt = {}, {}, {}
+        final_pair = PAIR_ORDER[-1]
 
         def fetch_a(t):
-            pa[t] = keep.tile([P, W], F32, name="pa%d" % t, tag="late" if t == PACK - 1 else "pa%d" % t, align_bytes=64)
+            pa[t] = keep.tile([P, W], F32, name="pa%d" % t, align_bytes=64)
             nc.vector.tensor_copy(pa[t][:], y[t][:].indirect(n1_t[:]))
 
         def fetch_b(t):
@@ -132,143 +144,138 @@ def tile_picked_hcandbondstd_none_p_kernel(tc, x_words, x_scales, w1, gs, offs, 
             nc.vector.tensor_copy(pb[t][:], y[t][:].indirect(n2_t[:]))
 
         def put_sum(t):
-            dt[t] = keep.tile([P, S], F32, name="dt%d" % t)
+            dt[t] = keep.tile([P, S], F32, name="dt%d" % t, tag="dt%d" % (PAIR_ORDER[0] if t == final_pair else t))
             nc.vector.tensor_tensor(dt[t][:].indirect(n1_t[:]), pa[t][:], pb[t][:], ALU.add)
 
         def put_product(t):
             nc.vector.tensor_tensor(dt[t][:].indirect(n2_t[:]), pa[t][:], pb[t][:], ALU.mult)
-
-        def weigh(t):
-            for u in (1, 0):
-                src = dt[t][:, u * HALF : (u + 1) * HALF]
-                if t >= 2 and u == 1:
-                    nc.vector.tensor_scalar(z_grouped[u][:, :, t], src, gs_t[:, t : t + 1], None, ALU.mult)
+            for u, cols in ((1, UPPER), (0, LOWER)):
+                if t == final_pair and cols == UPPER:
+                    nc.vector.tensor_scalar(z_grouped[u][:, :, t], dt[t][:, cols], gs_t[:, t : t + 1], None, ALU.mult)
                 else:
-                    nc.scalar.activation(z_grouped[u][:, :, t], src, ACT.Copy, scale=gs_t[:, t : t + 1])
+                    nc.scalar.activation(z_grouped[u][:, :, t], dt[t][:, cols], ACT.Copy, scale=gs_t[:, t : t + 1])
 
-        fetch_a(0)
-        fetch_b(0)
-        for t in range(PACK):
-            if t + 1 < PACK:
-                fetch_a(t + 1)
+        fetch_a(PAIR_ORDER[0])
+        fetch_b(PAIR_ORDER[0])
+        for t, following in zip(PAIR_ORDER[:2], PAIR_ORDER[1:3]):
+            fetch_a(following)
             put_sum(t)
-            if t + 1 < PACK:
-                fetch_b(t + 1)
-            else:
-                weigh(t - 1)
+            fetch_b(following)
             put_product(t)
-            if t != PACK - 2:
-                weigh(t)
+        fetch_a(final_pair)
+        fetch_b(final_pair)
+        for put in (put_sum, put_product):
+            put(PAIR_ORDER[2])
+            put(final_pair)
 
-        c_codes = keep.tile([P, C], U32, name="c_codes", tag="late", align_bytes=64)
+        c_codes = keep.tile([P, C], U32, name="c_codes", tag="pa%d" % final_pair, align_bytes=64)
         nc.vector.tensor_copy(c_codes[:].rearrange("p (t m) -> p m t", t=PACK), c_words[:].rearrange("p (m t) -> p m t", t=PACK))
 
         z_codes = keep.tile([P, S], U32, name="z_codes", align_bytes=64)
-        z_plane = keep.tile([P, S], U8, name="z_plane", align_bytes=64)
-        for u in (1, 0):
-            cols = slice(u * HALF, (u + 1) * HALF)
-            nc.vector.quantize_mx(z_codes[:, cols].bitcast(FP8X4), z_plane[:, cols], z_grouped[u][:].rearrange("p n t -> p (n t)"))
-
-        def scores(bank, t, cols):
-            rows = slice(t * P, (t + 1) * P)
-            nc.tensor.matmul_mx(bank, lhsT=c_codes[:, rows].bitcast(FP8X4), lhsT_scale=c_plane[:, rows],
-                                rhs=z_codes[:, cols].bitcast(FP8X4), rhs_scale=z_plane[:, cols], start=True, stop=True)
+        z_scale = keep.tile([P, S], U8, name="z_scale", align_bytes=64)
+        for u, cols in ((1, UPPER), (0, LOWER)):
+            nc.vector.quantize_mx(z_codes[:, cols].bitcast(FP8X4), z_scale[:, cols], z_grouped[u][:].rearrange("p n t -> p (n t)"))
 
         windows = [keep.tile([P, S], F32, name="window%d" % t) for t in range(PACK)]
-        selfs = [keep.tile([P, S], F32, name="self%d" % t) for t in range(PACK)]
+        owns = [keep.tile([P, S], F32, name="own%d" % t) for t in range(PACK)]
         rests = {0: keep.tile([P, S], F32, name="rest0")}
-        bank_upper = bank_tile(4, "s_upper", HALF)
-        scores(bank_upper[:], 0, upper)
-        bank_lower = bank_tile(3, "s_lower", HALF)
-        scores(bank_lower[:], 0, lower)
-        banks = {}
+        s_upper = bank_tile(4, "s_upper", HALF)
+        product(s_upper, c_codes, c_scale, 0, z_codes, z_scale, UPPER)
+        s_lower = bank_tile(3, "s_lower", HALF)
+        product(s_lower, c_codes, c_scale, 0, z_codes, z_scale, LOWER)
+        s_banks = {}
         for t in range(1, PACK):
-            banks[t] = bank_tile(4 + t, "s_bank")
-            scores(banks[t][:], t, slice(0, S))
-        nc.vector.tensor_scalar(windows[0][:, upper], bank_upper[:], OWN, None, ALU.mult)
-        nc.scalar.activation(windows[0][:, lower], bank_lower[:], ACT.Copy, scale=OWN)
-        nc.vector.tensor_scalar(selfs[0][:, upper], bank_upper[:], SELF, None, ALU.mult)
-        nc.scalar.activation(selfs[0][:, lower], bank_lower[:], ACT.Copy, scale=SELF)
-        nc.scalar.activation(rests[0][:, upper], bank_upper[:], ACT.Copy, scale=REST)
-        nc.scalar.activation(rests[0][:, lower], bank_lower[:], ACT.Copy, scale=REST)
-
+            s_banks[t] = bank_tile(PACK + t, "s_bank")
+            product(s_banks[t], c_codes, c_scale, t, z_codes, z_scale, WHOLE)
+        for tiles, scale in ((windows, WINDOW_SCALE), (owns, OWN_SCALE)):
+            nc.vector.tensor_scalar(tiles[0][:, UPPER], s_upper[:], scale, None, ALU.mult)
+            nc.scalar.activation(tiles[0][:, LOWER], s_lower[:], ACT.Copy, scale=scale)
+        for bank, cols in ((s_upper, UPPER), (s_lower, LOWER)):
+            nc.scalar.activation(rests[0][:, cols], bank[:], ACT.Copy, scale=REST_SHARE * WINDOW_SCALE)
         for t in range(1, PACK):
-            for tiles, scale in ((windows, OWN), (selfs, SELF)):
-                nc.scalar.activation(tiles[t][:], banks[t][:], ACT.Copy, scale=scale)
+            for tiles, scale in ((windows, WINDOW_SCALE), (owns, OWN_SCALE)):
+                nc.scalar.activation(tiles[t][:], s_banks[t][:], ACT.Copy, scale=scale)
 
         out_rows = out.rearrange("(p t) n -> t p n", t=PACK)
         firsts = [keep.tile([P, S], F32, name="first%d" % t) for t in range(PACK)]
         parts = [keep.tile([P, S], F32, name="part%d" % t) for t in range(PACK)]
-        nums = {}
-
-        def offsets(tile, cols):
-            return tile[:, cols.start // 16 : cols.stop // 16]
+        nums, invs = {}, {}
+        last = PACK - 1
 
         def look_up(t):
-            nums[t] = ring.tile([P, S], F32, name="num", bufs=3)
-            for cols in (upper, lower):
-                nc.vector.tensor_tensor(firsts[t][:, cols], windows[t][:].indirect(offsets(n3_t, cols)), selfs[t][:, cols], ALU.subtract)
-            for cols in (upper, lower):
+            nums[t] = ring.tile([P, S], F32, name="num")
+            for cols in (UPPER, LOWER):
+                nc.vector.tensor_tensor(firsts[t][:, cols], windows[t][:].indirect(offsets(n3_t, cols)), owns[t][:, cols], ALU.subtract)
+            for cols in (UPPER, LOWER):
                 nc.vector.tensor_tensor(nums[t][:, cols], windows[t][:].indirect(offsets(n4_t, cols)), firsts[t][:, cols], ALU.add)
-            for cols in (upper, lower):
+            for cols in (UPPER, LOWER):
                 nc.vector.scalar_tensor_tensor(parts[t][:, cols], firsts[t][:, cols], 2.0, nums[t][:, cols], ALU.mult, ALU.subtract)
 
-        invs = {}
-        whole = slice(0, S)
-
-        def turn_and_add(total, left, right, blocks):
-            for b in blocks:
+        def turn_and_add(total, left, right):
+            for b in range(HALF // P):
                 block = slice(b * P, (b + 1) * P)
-                place = slice(b * P % total.shape[1], b * P % total.shape[1] + P)
-                nc.tensor.matmul(total[:, place], lhsT=left[:, block], rhs=ident[:], is_transpose=True, start=True, stop=False)
-                nc.tensor.matmul(total[:, place], lhsT=right[:, block], rhs=ident[:], is_transpose=True, start=False, stop=True)
+                nc.tensor.matmul(total[:, block], lhsT=left[:, block], rhs=ident[:], is_transpose=True, start=True, stop=False)
+                nc.tensor.matmul(total[:, block], lhsT=right[:, block], rhs=ident[:], is_transpose=True, start=False, stop=True)
 
         def spread_on_tensor(t):
-            mean = bank_tile(0, "mean")
-            turn_and_add(mean, nums[t], rests[t], (2, 3, 0, 1))
-            mean2 = ring.tile([P, S], F32, name="mean2", bufs=1)
-            nc.scalar.activation(mean2[:], mean[:], ACT.Square, scale=MEAN)
-            diff2 = ring.tile([P, S], F32, name="diff2", bufs=1)
-            for u, cols in ((1, upper), (0, lower)):
-                diff = bank_tile(1 + u, "diff", HALF)
-                turn_and_add(diff, parts[t], selfs[t], (2 * u, 2 * u + 1))
-                nc.scalar.activation(diff2[:, cols], diff[:], ACT.Square, scale=DIFF)
-            if t + 1 < PACK - 1:
+            mean = bank_tile(MEAN_BANK, "mean")
+            for cols in (UPPER, LOWER):
+                turn_and_add(mean[:, cols], nums[t][:, cols], rests[t][:, cols])
+            mean2 = keep.tile([P, S], F32, name="mean2")
+            nc.scalar.activation(mean2[:], mean[:], ACT.Square, scale=MEAN_SCALE)
+            diff2 = {}
+            for u, cols in ((1, UPPER), (0, LOWER)):
+                diff = bank_tile(DIFF_BANK + u, "diff", HALF)
+                turn_and_add(diff[:], parts[t][:, cols], owns[t][:, cols])
+                diff2[u] = keep.tile([P, HALF], F32, name="diff2_%d" % u)
+                nc.scalar.activation(diff2[u][:], diff[:], ACT.Square, scale=DIFF_SCALE)
+            if t + 1 < last:
                 rests[t + 1] = keep.tile([P, S], F32, name="rest%d" % (t + 1), tag="part%d" % t)
-                nc.scalar.activation(rests[t + 1][:], banks[t + 1][:], ACT.Copy, scale=REST)
-            den = bank_tile(3, "den")
-            turn_and_add(den, mean2, diff2, (2, 3, 0, 1))
-            invs[t] = ring.tile([P, S], F32, name="inv")
+                nc.scalar.activation(rests[t + 1][:], s_banks[t + 1][:], ACT.Copy, scale=REST_SHARE * WINDOW_SCALE)
+            den = bank_tile(DEN_BANK, "den")
+            for u, cols in ((1, UPPER), (0, LOWER)):
+                turn_and_add(den[:, cols], mean2[:, cols], diff2[u][:])
+            return den
+
+        def invert(t, den, tag):
+            invs[t] = keep.tile([P, S], F32, name="inv%d" % t, tag=tag)
             nc.scalar.activation(invs[t][:], den[:], ACT.Abs_reciprocal_sqrt, bias=0.25)
 
-        def spread_on_vector(t):
+        def squares_on_vector(t):
             mean = keep.tile([P, S], F32, name="mean_last")
-            nc.vector.scalar_tensor_tensor(mean[:], windows[t][:], 8 / 15, nums[t][:], ALU.mult, ALU.add)
-            mean2 = ring.tile([P, S], F32, name="mean2", bufs=1)
-            nc.scalar.activation(mean2[:], mean[:], ACT.Square, scale=MEAN)
+            nc.vector.scalar_tensor_tensor(mean[:], windows[t][:], REST_SHARE, nums[t][:], ALU.mult, ALU.add)
+            squares = keep.tile([P, 2 * S], F32, name="squares_last", tag="diff2_1")
+            mean2, diff2 = squares[:, :S], squares[:, S:]
+            nc.scalar.activation(mean2, mean[:], ACT.Square, scale=MEAN_SCALE)
             diff = keep.tile([P, S], F32, name="diff_last")
-            diff2 = ring.tile([P, S], F32, name="diff2", bufs=1)
-            for cols in (upper, lower):
-                nc.vector.tensor_tensor(diff[:, cols], parts[t][:, cols], selfs[t][:, cols], ALU.add)
-                nc.scalar.activation(diff2[:, cols], diff[:, cols], ACT.Square, scale=DIFF)
-            finish(t - 2, whole)
+            for cols in (UPPER, LOWER):
+                nc.vector.tensor_tensor(diff[:, cols], parts[t][:, cols], owns[t][:, cols], ALU.add)
+                nc.scalar.activation(diff2[:, cols], diff[:, cols], ACT.Square, scale=DIFF_SCALE)
+            return mean2, diff2
+
+        def invert_on_vector(t, mean2, diff2):
             den = keep.tile([P, S], F32, name="den_last")
-            invs[t] = ring.tile([P, S], F32, name="inv")
-            for cols in (upper, lower):
+            invs[t] = keep.tile([P, S], F32, name="inv%d" % t)
+            for cols in (UPPER, LOWER):
                 nc.vector.tensor_tensor(den[:, cols], mean2[:, cols], diff2[:, cols], ALU.add)
                 nc.scalar.activation(invs[t][:, cols], den[:, cols], ACT.Abs_reciprocal_sqrt, bias=0.25)
 
         def finish(t, cols):
-            res = ring.tile([P, cols.stop - cols.start], F32, name="res")
-            nc.vector.tensor_tensor(res[:], nums[t][:, cols], invs[t][:, cols], ALU.mult)
-            nc.sync.dma_start(out_rows[t][:, cols], res[:])
+            result = ring.tile([P, cols.stop - cols.start], F32, name="result")
+            nc.vector.tensor_tensor(result[:], nums[t][:, cols], invs[t][:, cols], ALU.mult)
+            nc.sync.dma_start(out_rows[t][:, cols], result[:])
 
-        for t in range(PACK - 1):
+        for t in range(last - 1):
             look_up(t)
-            spread_on_tensor(t)
-        finish(0, whole)
-        look_up(PACK - 1)
-        spread_on_vector(PACK - 1)
-        finish(PACK - 2, whole)
-        finish(PACK - 1, upper)
-        finish(PACK - 1, lower)
+            invert(t, spread_on_tensor(t), "inv%d" % t)
+        look_up(last - 1)
+        den_before_last = spread_on_tensor(last - 1)
+        finish(0, WHOLE)
+        look_up(last)
+        last_squares = squares_on_vector(last)
+        finish(1, WHOLE)
+        invert(last - 1, den_before_last, "diff_last")
+        invert_on_vector(last, *last_squares)
+        finish(last - 1, WHOLE)
+        finish(last, UPPER)
+        finish(last, LOWER)

import math
from contextlib import ExitStack

import concourse.mybir as mybir
from concourse.masks import make_identity

K, T, S, H, W, C = 512, 2048, 512, 512, 256, 512
FLOPS = 2 * K * H * S + 2 * K * C * S

F32 = mybir.dt.float32
BF16 = mybir.dt.bfloat16
I32 = mybir.dt.int32
U32 = mybir.dt.uint32
U16 = mybir.dt.uint16
U8 = mybir.dt.uint8
FP8X4 = mybir.dt.float8_e4m3fn_x4
ALU = mybir.AluOpType
ACT = mybir.ActivationFunctionType

P = 128
PACK = 4
GROUP = 16
QUADRANT = 32
HALF = S // 2
LOWER, UPPER, WHOLE = slice(0, HALF), slice(HALF, S), slice(0, S)
PAIR_ORDER = (2, 0, 1, 3)
W_PIECES = ((0, 128), (128, 256), (256, 512))
WINDOW_SCALE = -0.3125 * 0.0625
OWN_SCALE = 2.2 * WINDOW_SCALE
REST_SHARE = 8 / 15
MEAN_SCALE = math.sqrt(0.5) * 1.2
DIFF_SCALE = math.sqrt(0.5) * 3.2
MEAN_BANK, DIFF_BANK, DEN_BANK = 0, 1, 3


def tile_picked_hcandbondstd_none_p_kernel(tc, x_words, x_scales, w1, gs, offs, n1, n2, cand, n3, n4, out):
    nc = tc.nc
    with ExitStack() as ctx:
        keep = ctx.enter_context(tc.tile_pool(name="keep", bufs=1))
        ring = ctx.enter_context(tc.tile_pool(name="ring", bufs=3))
        psum = ctx.enter_context(tc.psum_pool(name="psum", bufs=1))

        def load_list(dram, name):
            tile = keep.tile(list(dram.shape), U16, name=name)
            nc.sync.dma_start(tile[:], dram)
            return tile

        def offsets(tile, cols):
            return tile[:, cols.start // GROUP : cols.stop // GROUP]

        def bank_tile(b, name, width=S):
            return psum.tile([P, width], F32, name=name, tag="bank%d" % b)

        def product(bank, lhs_codes, lhs_scales, t, rhs_codes, rhs_scales, cols):
            rows = slice(t * P, (t + 1) * P)
            nc.tensor.matmul_mx(bank[:], lhsT=lhs_codes[:, rows].bitcast(FP8X4), lhsT_scale=lhs_scales[:, rows],
                                rhs=rhs_codes[:, cols].bitcast(FP8X4), rhs_scale=rhs_scales[:, cols], start=True, stop=True)

        table_scales = keep.tile([P, T], U8, name="table_scales")
        nc.gpsimd.memset(table_scales[:].bitcast(I32), 0)
        one = keep.tile([P, 1], F32, name="one")
        nc.vector.memset(one[:], 1.0)
        preload = keep.tile([P, 1], F32, name="preload")
        nc.scalar.activation(preload[:], one[:], ACT.Abs_reciprocal_sqrt)

        offs_t = load_list(offs, "offs_t")
        cand_t = load_list(cand, "cand_t")
        w_rows = w1.rearrange("(p j) h -> p j h", j=PACK)
        w_raw = []
        for n, (lo, hi) in enumerate(W_PIECES):
            piece = keep.tile([P, PACK, hi - lo], F32, name="w_raw%d" % n)
            nc.sync.dma_start(piece[:], w_rows[:, :, lo:hi])
            w_raw.append(piece)
            if n == 0:
                scale_rows = x_scales[0].rearrange("(r e) n -> e r n", e=2)
                for e in range(2):
                    nc.sync.dma_start(table_scales[e:P:GROUP, :].bitcast(I32), scale_rows[e].bitcast(I32))
        table_words = keep.tile([P, T], U32, name="table_words")
        nc.sync.dma_start(table_words[:].bitcast(I32), x_words[0].rearrange("p n t -> p (n t)").bitcast(I32))
        n1_t = load_list(n1, "n1_t")
        n2_t = load_list(n2, "n2_t")
        n3_t = load_list(n3, "n3_t")
        n4_t = load_list(n4, "n4_t")
        gs_t = keep.tile([P, PACK], F32, name="gs_t")
        nc.sync.dma_start(gs_t[:], gs.rearrange("(p t) o -> p (t o)", t=PACK))
        ident = keep.tile([P, P], F32, name="ident")
        make_identity(nc, ident[:])

        def move_scale_row(dst, src, row):
            gathered_at = GROUP * (row // 2) + row % 2
            nc.sync.dma_start(dst[row:P:QUADRANT, :].bitcast(I32), src[gathered_at:P:QUADRANT, :].bitcast(I32))

        x_bytes = keep.tile([P, S], U8, name="x_bytes")
        nc.vector.tensor_copy(x_bytes[:], table_scales[:].indirect(offs_t[:]))
        x_scale = keep.tile([P, S], U8, name="x_scale", align_bytes=64)
        nc.vector.tensor_copy(x_scale[:].bitcast(I32), x_bytes[:].bitcast(I32))
        for row in (2, 3):
            move_scale_row(x_scale, x_bytes, row)

        c_bytes = keep.tile([P, C], U8, name="c_bytes")
        nc.vector.tensor_copy(c_bytes[:], table_scales[:].indirect(cand_t[:]))
        c_bytes_dealt = keep.tile([P, C], U8, name="c_bytes_dealt")
        nc.vector.tensor_copy(c_bytes_dealt[:].rearrange("p (t m) -> p t m", t=PACK), c_bytes[:].rearrange("p (m t) -> p t m", t=PACK))
        c_scale = keep.tile([P, C], U8, name="c_scale", align_bytes=64)
        nc.gpsimd.memset(c_scale[:].bitcast(I32), 0)
        for row in range(4):
            move_scale_row(c_scale, c_bytes_dealt, row)

        w_grouped = keep.tile([P, PACK, P, PACK], BF16, name="w_grouped", align_bytes=64)
        for n, (lo, hi) in enumerate(W_PIECES):
            nc.scalar.copy(w_grouped[:, :, lo // PACK : hi // PACK, :].rearrange("p t m j -> p m t j"),
                           w_raw[n][:].rearrange("p j (m t) -> p m t j", t=PACK))
        w_codes = keep.tile([P, H], U32, name="w_codes", align_bytes=64)
        w_scale = keep.tile([P, H], U8, name="w_scale", align_bytes=64)
        nc.vector.quantize_mx(w_codes[:].bitcast(FP8X4), w_scale[:], w_grouped[:].rearrange("p t m j -> p (t m j)"))

        x_codes = keep.tile([P, S], U32, name="x_codes", align_bytes=64)
        for cols in (LOWER, UPPER):
            nc.vector.tensor_copy(x_codes[:, cols], table_words[:].indirect(offsets(offs_t, cols)))

        y = [keep.tile([P, S], F32, name="y%d" % t) for t in range(PACK)]
        for b, cols in ((PAIR_ORDER[0], LOWER), (PACK, UPPER)):
            bank = bank_tile(b, "y_half", HALF)
            product(bank, w_codes, w_scale, PAIR_ORDER[0], x_codes, x_scale, cols)
            nc.scalar.copy(y[PAIR_ORDER[0]][:, cols], bank[:])
        for t in PAIR_ORDER[1:]:
            bank = bank_tile(t, "y_bank")
            product(bank, w_codes, w_scale, t, x_codes, x_scale, WHOLE)
            nc.scalar.copy(y[t][:], bank[:])

        c_words = keep.tile([P, C], U32, name="c_words")
        nc.vector.tensor_copy(c_words[:], table_words[:].indirect(cand_t[:]))

        z_grouped = [keep.tile([P, HALF, PACK], BF16, name="z_grouped%d" % u, align_bytes=64) for u in range(2)]
        pa, pb, dt = {}, {}, {}
        final_pair = PAIR_ORDER[-1]

        def fetch_a(t):
            pa[t] = keep.tile([P, W], F32, name="pa%d" % t, align_bytes=64)
            nc.vector.tensor_copy(pa[t][:], y[t][:].indirect(n1_t[:]))

        def fetch_b(t):
            pb[t] = keep.tile([P, W], F32, name="pb%d" % t)
            nc.vector.tensor_copy(pb[t][:], y[t][:].indirect(n2_t[:]))

        def put_sum(t):
            dt[t] = keep.tile([P, S], F32, name="dt%d" % t, tag="dt%d" % (PAIR_ORDER[0] if t == final_pair else t))
            nc.vector.tensor_tensor(dt[t][:].indirect(n1_t[:]), pa[t][:], pb[t][:], ALU.add)

        def put_product(t):
            nc.vector.tensor_tensor(dt[t][:].indirect(n2_t[:]), pa[t][:], pb[t][:], ALU.mult)
            for u, cols in ((1, UPPER), (0, LOWER)):
                if t == final_pair and cols == UPPER:
                    nc.vector.tensor_scalar(z_grouped[u][:, :, t], dt[t][:, cols], gs_t[:, t : t + 1], None, ALU.mult)
                else:
                    nc.scalar.activation(z_grouped[u][:, :, t], dt[t][:, cols], ACT.Copy, scale=gs_t[:, t : t + 1])

        fetch_a(PAIR_ORDER[0])
        fetch_b(PAIR_ORDER[0])
        for t, following in zip(PAIR_ORDER[:2], PAIR_ORDER[1:3]):
            fetch_a(following)
            put_sum(t)
            fetch_b(following)
            put_product(t)
        fetch_a(final_pair)
        fetch_b(final_pair)
        for put in (put_sum, put_product):
            put(PAIR_ORDER[2])
            put(final_pair)

        c_codes = keep.tile([P, C], U32, name="c_codes", tag="pa%d" % final_pair, align_bytes=64)
        nc.vector.tensor_copy(c_codes[:].rearrange("p (t m) -> p m t", t=PACK), c_words[:].rearrange("p (m t) -> p m t", t=PACK))

        z_codes = keep.tile([P, S], U32, name="z_codes", align_bytes=64)
        z_scale = keep.tile([P, S], U8, name="z_scale", align_bytes=64)
        for u, cols in ((1, UPPER), (0, LOWER)):
            nc.vector.quantize_mx(z_codes[:, cols].bitcast(FP8X4), z_scale[:, cols], z_grouped[u][:].rearrange("p n t -> p (n t)"))

        windows = [keep.tile([P, S], F32, name="window%d" % t) for t in range(PACK)]
        owns = [keep.tile([P, S], F32, name="own%d" % t) for t in range(PACK)]
        rests = {0: keep.tile([P, S], F32, name="rest0")}
        s_upper = bank_tile(4, "s_upper", HALF)
        product(s_upper, c_codes, c_scale, 0, z_codes, z_scale, UPPER)
        s_lower = bank_tile(3, "s_lower", HALF)
        product(s_lower, c_codes, c_scale, 0, z_codes, z_scale, LOWER)
        s_banks = {}
        for t in range(1, PACK):
            s_banks[t] = bank_tile(PACK + t, "s_bank")
            product(s_banks[t], c_codes, c_scale, t, z_codes, z_scale, WHOLE)
        for tiles, scale in ((windows, WINDOW_SCALE), (owns, OWN_SCALE)):
            nc.vector.tensor_scalar(tiles[0][:, UPPER], s_upper[:], scale, None, ALU.mult)
            nc.scalar.activation(tiles[0][:, LOWER], s_lower[:], ACT.Copy, scale=scale)
        for bank, cols in ((s_upper, UPPER), (s_lower, LOWER)):
            nc.scalar.activation(rests[0][:, cols], bank[:], ACT.Copy, scale=REST_SHARE * WINDOW_SCALE)
        for t in range(1, PACK):
            for tiles, scale in ((windows, WINDOW_SCALE), (owns, OWN_SCALE)):
                nc.scalar.activation(tiles[t][:], s_banks[t][:], ACT.Copy, scale=scale)

        out_rows = out.rearrange("(p t) n -> t p n", t=PACK)
        firsts = [keep.tile([P, S], F32, name="first%d" % t) for t in range(PACK)]
        parts = [keep.tile([P, S], F32, name="part%d" % t) for t in range(PACK)]
        nums, invs = {}, {}
        last = PACK - 1

        def look_up(t):
            nums[t] = ring.tile([P, S], F32, name="num")
            for cols in (UPPER, LOWER):
                nc.vector.tensor_tensor(firsts[t][:, cols], windows[t][:].indirect(offsets(n3_t, cols)), owns[t][:, cols], ALU.subtract)
            for cols in (UPPER, LOWER):
                nc.vector.tensor_tensor(nums[t][:, cols], windows[t][:].indirect(offsets(n4_t, cols)), firsts[t][:, cols], ALU.add)
            for cols in (UPPER, LOWER):
                nc.vector.scalar_tensor_tensor(parts[t][:, cols], firsts[t][:, cols], 2.0, nums[t][:, cols], ALU.mult, ALU.subtract)

        def turn_and_add(total, left, right):
            for b in range(HALF // P):
                block = slice(b * P, (b + 1) * P)
                nc.tensor.matmul(total[:, block], lhsT=left[:, block], rhs=ident[:], is_transpose=True, start=True, stop=False)
                nc.tensor.matmul(total[:, block], lhsT=right[:, block], rhs=ident[:], is_transpose=True, start=False, stop=True)

        def spread_on_tensor(t):
            mean = bank_tile(MEAN_BANK, "mean")
            for cols in (UPPER, LOWER):
                turn_and_add(mean[:, cols], nums[t][:, cols], rests[t][:, cols])
            mean2 = keep.tile([P, S], F32, name="mean2")
            nc.scalar.activation(mean2[:], mean[:], ACT.Square, scale=MEAN_SCALE)
            diff2 = {}
            for u, cols in ((1, UPPER), (0, LOWER)):
                diff = bank_tile(DIFF_BANK + u, "diff", HALF)
                turn_and_add(diff[:], parts[t][:, cols], owns[t][:, cols])
                diff2[u] = keep.tile([P, HALF], F32, name="diff2_%d" % u)
                nc.scalar.activation(diff2[u][:], diff[:], ACT.Square, scale=DIFF_SCALE)
            if t + 1 < last:
                rests[t + 1] = keep.tile([P, S], F32, name="rest%d" % (t + 1), tag="part%d" % t)
                nc.scalar.activation(rests[t + 1][:], s_banks[t + 1][:], ACT.Copy, scale=REST_SHARE * WINDOW_SCALE)
            den = bank_tile(DEN_BANK, "den")
            for u, cols in ((1, UPPER), (0, LOWER)):
                turn_and_add(den[:, cols], mean2[:, cols], diff2[u][:])
            return den

        def invert(t, den, tag):
            invs[t] = keep.tile([P, S], F32, name="inv%d" % t, tag=tag)
            nc.scalar.activation(invs[t][:], den[:], ACT.Abs_reciprocal_sqrt, bias=0.25)

        def squares_on_vector(t):
            mean = keep.tile([P, S], F32, name="mean_last")
            nc.vector.scalar_tensor_tensor(mean[:], windows[t][:], REST_SHARE, nums[t][:], ALU.mult, ALU.add)
            squares = keep.tile([P, 2 * S], F32, name="squares_last", tag="diff2_1")
            mean2, diff2 = squares[:, :S], squares[:, S:]
            nc.scalar.activation(mean2, mean[:], ACT.Square, scale=MEAN_SCALE)
            diff = keep.tile([P, S], F32, name="diff_last")
            for cols in (UPPER, LOWER):
                nc.vector.tensor_tensor(diff[:, cols], parts[t][:, cols], owns[t][:, cols], ALU.add)
                nc.scalar.activation(diff2[:, cols], diff[:, cols], ACT.Square, scale=DIFF_SCALE)
            return mean2, diff2

        def invert_on_vector(t, mean2, diff2):
            den = keep.tile([P, S], F32, name="den_last")
            invs[t] = keep.tile([P, S], F32, name="inv%d" % t)
            for cols in (UPPER, LOWER):
                nc.vector.tensor_tensor(den[:, cols], mean2[:, cols], diff2[:, cols], ALU.add)
                nc.scalar.activation(invs[t][:, cols], den[:, cols], ACT.Abs_reciprocal_sqrt, bias=0.25)

        def finish(t, cols):
            result = ring.tile([P, cols.stop - cols.start], F32, name="result")
            nc.vector.tensor_tensor(result[:], nums[t][:, cols], invs[t][:, cols], ALU.mult)
            nc.sync.dma_start(out_rows[t][:, cols], result[:])

        for t in range(last - 1):
            look_up(t)
            invert(t, spread_on_tensor(t), "inv%d" % t)
        look_up(last - 1)
        den_before_last = spread_on_tensor(last - 1)
        finish(0, WHOLE)
        look_up(last)
        last_squares = squares_on_vector(last)
        finish(1, WHOLE)
        invert(last - 1, den_before_last, "diff_last")
        invert_on_vector(last, *last_squares)
        finish(last - 1, WHOLE)
        finish(last, UPPER)
        finish(last, LOWER)
